import numpy as np, ml_dtypes
CORES = [16,18,20,22]
N = 4
BF = ml_dtypes.bfloat16
L, XS, PS, VIS, ST, SH = 256, 16, 4, 5, 1, 5
W, PN = L * XS, L * PS
def pack(x, z, c, p, q, t, w, d):
    b = lambda a: np.ascontiguousarray(a.reshape(N, 128, -1)).astype(np.float32).astype(BF)
    i = lambda a: np.ascontiguousarray(a.reshape(N, 128, -1)).astype(np.int32)
    return {"xt": b(x), "zt": b(z), "ch": i(c), "pa": i(p), "vi": i(q), "pl": i(t), "wt": i(w), "de": i(np.repeat(d.reshape(N, 8, 1), 16, axis=2))}
def parts(rng):
    top = rng.choice(np.array([3, 15, 255, 255]), (N, 8, 1, 1))
    x = rng.integers(0, top + 1, (N, 8, 16, W)); z = rng.integers(0, 256, (N, 8, 16, L))
    c, p, q = (rng.integers(0, W, (N, 8, 16, L)) for a in range(3)); q = np.where(rng.random(q.shape) < 0.1, p, q)
    t = rng.integers(0, W, (N, 8, 16, PN)); w = rng.integers(0, 256, (N, 8, 16)); d = rng.integers(3, 8, (N, 8))
    return x, z, c, p, q, t, w, d
def plant(rng, x, z, c, p, q, a, g, s):
    h = W // 2; o = rng.permutation(W); back = 37 * np.arange(16)[:, None]
    x[a, g][:, o[:h]] = rng.integers(0, 11, (16, h)); x[a, g][:, o[h:]] = rng.integers(245, 256, (16, h)); z[a, g] = 0
    e = rng.integers(0, 2, (1, L)); own, near, far = (o[rng.integers(0, h, (16, L)) + h * v] for v in (e, e, 1 - e))
    pc = np.where(s < 0, far, near); qc = np.where(s > 0, far, near)
    c[a, g] = (own - back) & (W - 1); p[a, g] = (pc - back) & (W - 1); q[a, g] = (qc - back) & (W - 1)
def small(rng, x, c, p, q, t, w, d, a, g, n):
    b = (a - ST) % N; k = np.arange(16); m = int(rng.integers(3, 7)); d[a, g] = m; w[a, g] = 0
    x[a] = x[a][:, :, :1].copy(); o = XS * int(rng.integers(0, L)) + 1; x[a, g][:, o] = 255 - x[a, g][:, o]
    hit = (o - 37 * k) & (W - 1)
    def plain(v):
        return (XS * rng.integers(0, L, (16, v)) + rng.integers(2, XS, (16, v)) - 37 * k[:, None]) & (W - 1)
    c[a, g] = plain(L); p[a, g] = plain(L); q[a, g] = plain(L); t[a, g][:, :1] = plain(1)
    lanes = 1 + rng.permutation(L - 1)[:3 * n]
    for j in range(3 * n):
        l = int(lanes[j]); r = m + (1 if j >= 2 * n else 0); st = int(rng.integers(0, 17 - r)); on = (k >= st) & (k < st + r)
        c[a, g][on, l] = hit[on]
        if j < n: q[a, g][on, l] = hit[on]
        else:
            s = np.where(on, hit, plain(1)[:, 0])
            for v in (c, p, q): v[b, g][:, l] = s
def atends(rng, hi, shape, share):
    col = rng.integers(0, 2, shape[:-2] + (1, shape[-1])); el = rng.integers(0, 2, shape)
    v = np.where(rng.random(col.shape) < 0.5, col, el) * hi
    return np.where(rng.random(shape) < share, v, rng.integers(0, hi + 1, shape))
def setup_inputs(rng):
    return pack(*parts(rng))
def setup_inputs_spread(rng):
    x, z, c, p, q, t, w, d = parts(rng)
    x = (np.exp2(8 * rng.random((N, 8, 1, W))) * rng.random((N, 8, 16, W))).astype(np.int64)
    z = (np.exp2(8 * rng.random((N, 8, 1, L))) * rng.random((N, 8, 16, L))).astype(np.int64)
    def un(shape):
        v = np.minimum(np.exp2(12 * rng.random(shape)).astype(np.int64), W) - 1
        return np.where(rng.random(shape) < 0.5, v, W - 1 - v)
    c, p, q, t = un(c.shape), un(p.shape), un(q.shape), un(t.shape)
    w = np.minimum(np.exp2(8 * rng.random(w.shape)).astype(np.int64), 256) - 1; d = np.minimum(np.exp2(4 * rng.random(d.shape)).astype(np.int64), 16)
    return pack(x, z, c, p, q, t, w, d)
def setup_inputs_ends(rng):
    x = atends(rng, 255, (N, 8, 16, W), 1.0); z = atends(rng, 255, (N, 8, 16, L), 1.0)
    one = (rng.integers(0, 16, (N, 8, 1, W)) == np.arange(16).reshape(1, 1, 16, 1)) & (rng.random((N, 8, 1, W)) < 0.3)
    x = np.where(one, np.abs(x - 1), x)
    c, p, q = (atends(rng, W - 1, (N, 8, 16, L), 0.75) for a in range(3)); t = atends(rng, W - 1, (N, 8, 16, PN), 0.85)
    w = rng.integers(0, 2, (N, 8, 16)) * 255; w[:, 1, ::2] = 0; w[:, 2] = 255; w[:, 7] = 255
    d = np.where(rng.random((N, 8)) < 0.6, 1, 16); d[:, 0] = 1; d[:, 7] = 16; d[N - 1, 2] = 16
    k = np.arange(16); hx = (37 * k) & (W - 1); hy = (((W - 1) ** 2 >> SH) + W - 1 + 37 * k) & (W - 1)
    item = np.zeros(16, np.int64); item[0] = 255; item[1] = 2
    for a in range(N):
        for g in (2, 7):
            if (a + g + N) % 2 == 0: x[a, g][:, hx] = item[:, None]; x[a, g][:, hy] = np.where(item > 0, 0, 255)[:, None]
            else: x[a, g][:, hx] = 255; x[a, g][:, hy] = 0
            for l in (2, 5, L - 1, 3, L - 2):
                down = l in (2, 5, L - 1); z[a, g][:, l] = item; c[a, g][:, l] = 0
                p[a, g][:, l] = W - 1 if down else 0; q[a, g][:, l] = 0 if down else W - 1
            up = (((4093 * 4075) >> SH) + 4093 + 37 * k) & (W - 1)
            x[a, g][:, up + 1] = x[a, g][:, hx]; x[a, g][:, up] = x[a, g][:, hy]
            for l, nc, nr, nq in ((8, 0, 4093, 0), (11, 4093, 0, 4093), (14, 0, 0, 4093), (L - 4, 0, 4093, 0), (L - 7, 4093, 0, 4093)):
                z[a, g][:, l] = 0; z[a, g][:5, l] = 255; z[a, g][5, l] = 26
                c[a, g][:, l] = nc; p[a, g][:, l] = nr; q[a, g][:, l] = nq
    return pack(x, z, c, p, q, t, w, d)
def setup_inputs_corners(rng):
    x, z, c, p, q, t, w, d = parts(rng); k = np.arange(16)[:, None]
    tie = np.array([0, 0, -1, -1, 0, 0, 1, 1, 0, -1, -1, 0, 1, 1, 0, 1])
    for a in range(N):
        for g in range(8):
            case = (g + a) % 8
            if a == 1: case = (0, 2)[g % 2]
            if a == 2: case = (1, 3, 4)[g % 3]
            if a > 2 and a % 2 == 1 and case == 7: case = 0
            n = int(rng.integers(2, 8)); st = rng.integers(0, 17 - n, (1, L)); s = np.full((16, L), -1); d[a, g] = 16
            if case < 2: s = np.where((k >= st) & (k < st + n), -1, 1); d[a, g] = n + case
            if case == 3: s = np.full((16, L), 1); d[a, g] = 1
            if case == 4: s = np.zeros((16, L), np.int64); d[a, g] = 1
            if case == 5: s = tie[(k + rng.integers(0, 16, (1, L))) % 16]; d[a, g] = 2
            if case == 6: s = np.where(k == 15 * rng.integers(0, 2, (1, L)), -1, 1); d[a, g] = 1
            if case == 7: s[:, int(rng.integers(0, L))] = 0
            plant(rng, x, z, c, p, q, a, g, s)
            j = int(rng.integers(0, 4))
            if j == 0: w[a, g] = 0
            if j == 1: w[a, g] = 255
            if j == 2: w[a, g] = 0; w[a, g, int(rng.integers(0, 16))] = 1
    return pack(x, z, c, p, q, t, w, d)
def setup_inputs_crowd(rng):
    x, z, c, p, q, t, w, d = parts(rng); few = np.array([0, W - 1, W // 2, 3])
    for a in range(N):
        for g in range(8):
            if a in (0, 2):
                plant(rng, x, z, c, p, q, a, g, np.full((16, L), -1)); d[a, g] = int(rng.integers(3, 7))
                for v in (c, p, q): v[a, g] = v[a, g][:, :1].copy()
                if a == 2 and g == 7: l = int(rng.integers(0, L)); p[a, g][:, l] = c[a, g][:, l]; q[a, g][:, l] = c[a, g][:, l]
            elif g % 2 == 0:
                for v in (c, p, q): v[a, g] = rng.choice(few, (16, L))
                z[a, g] = z[a, g][:, rng.integers(0, 4, L)]
            else:
                t[a, g] = t[a, g][:, rng.integers(0, 3, PN)]
                if g == 3: x[a, g] = x[a, g][:, :1].copy()
                if g == 5: y = x[a, g][:, 1].copy(); x[a, g] = x[a, g][:, :1].copy(); x[a, g][:, int(rng.integers(0, W))] = y
    return pack(x, z, c, p, q, t, w, d)
def setup_inputs_close(rng):
    x, z, c, p, q, t, w, d = parts(rng); m = rng.integers(0, 256, (N, 8, 16, 1))
    x = np.where(rng.random((N, 8, 1, W)) < 0.5, m, 255 - m)
    e = (rng.integers(0, 16, (N, 8, 1, W)) == np.arange(16).reshape(1, 1, 16, 1)) * rng.integers(-1, 2, (N, 8, 1, W))
    x = np.clip(x + e, 0, 255); d = rng.integers(1, 6, (N, 8)); gs = rng.permutation(8)
    small(rng, x, c, p, q, t, w, d, 1, int(gs[0]), 1)
    small(rng, x, c, p, q, t, w, d, 3, int(gs[1]), 3)
    return pack(x, z, c, p, q, t, w, d)
def check_inputs(d):
    bad = []
    for k, lo, hi in (("xt", 0, 255), ("zt", 0, 255), ("ch", 0, W - 1), ("pa", 0, W - 1), ("vi", 0, W - 1), ("pl", 0, W - 1), ("wt", 0, 255), ("de", 1, 16)):
        v = np.asarray(d[k]).astype(np.float64)
        if not (np.min(v) >= lo and np.max(v) <= hi): bad.append("range of " + k)
        elif np.any(v != np.floor(v)): bad.append("whole numbers in " + k)
    v = np.asarray(d["de"]).reshape(N, 8, 16)
    if np.any(v != v[:, :, :1]): bad.append("de alike in a group")
    return bad
def reference(xt, zt, ch, pa, vi, pl, wt, de):
    x = xt.astype(np.float32).astype(np.int32).reshape(N, 8, 16, W); z = zt.astype(np.float32).astype(np.int64).reshape(N, 8, 16, L)
    c, p, q = (a.astype(np.int64).reshape(N, 8, 16, L) for a in (ch, pa, vi)); t = pl.astype(np.int64).reshape(N, 8, 16, PN)
    w = wt.astype(np.int64).reshape(N, 8, 16, 1); d = de.astype(np.int64).reshape(N, 8, 16)[:, :, :1]
    site = np.arange(16).reshape(1, 1, 16, 1); k = np.arange(16); lane = np.arange(L); count = np.zeros((N, 1, 1), np.int64)
    for visit in range(VIS):
        if visit > 0: q = np.roll(q, ST, axis=0)
        u = np.add.reduce(w * z, axis=2) & (W - 1)
        got = []
        for n in (c, p, q):
            h = (((n * u[:, :, None]) >> SH) + n + 37 * site) & (W - 1)
            ix = np.ascontiguousarray(h.transpose(0, 1, 3, 2)).reshape(N, 8, 1, 16 * L)
            got.append(np.take_along_axis(x, ix, 3).reshape(N, 8, 16, L, 16))
        xs, ys, vs = got
        s = np.sign(np.add.reduce(np.abs(xs - vs), axis=2) - np.add.reduce(np.abs(xs - ys), axis=2)).astype(np.int64)
        H = np.zeros((N, 8, L), np.int64); top = H; ti = H; best = H - 99; bi = H; bj = H
        for j in range(1, 17):
            H = H + s[..., j - 1]; e = top - H; win = e > best
            best = np.where(win, e, best); bi = np.where(win, ti, bi); bj = np.where(win, j, bj)
            ge = H >= top; top = np.where(ge, H, top); ti = np.where(ge, j, ti)
        run = (k >= bi[..., None]) & (k < bj[..., None])
        m = np.max(np.where(run[:, :, None], xs, 0), axis=4).astype(np.int64)
        um = np.add.reduce(w * m, axis=2) & (W - 1)
        rec = best >= d + (count & 1)
        cut = run.transpose(0, 1, 3, 2) & rec[:, :, None]
        c, q = np.where(cut, p, c), np.where(cut, c, q)
        p = np.take_along_axis(t, (um & (PN - 1))[:, :, None], 3)
        at = (PS * lane + (um & (PS - 1)))[:, :, None]
        np.put_along_axis(t, at, np.where(rec[:, :, None], c, np.take_along_axis(t, at, 3)), 3)
        ib = bi[:, :, None, :, None]
        xi = np.take_along_axis(xs, ib, 4)[..., 0]; vv = np.take_along_axis(vs, ib, 4)[..., 0]
        np.put_along_axis(x, (XS * lane + (um & (XS - 1)))[:, :, None], (xi + vv) >> 1, 3)
        z = (z + m) >> 1
        count = np.add.reduce(rec.reshape(N, 8 * L).astype(np.int64), axis=1).reshape(N, 1, 1)
    return {"yc": c.reshape(N, 128, L).astype(np.float32), "yp": p.reshape(N, 128, L).astype(np.float32), "yq": q.reshape(N, 128, L).astype(np.float32),
            "yl": t.reshape(N, 128, PN).astype(np.float32), "yx": x.reshape(N, 128, W).astype(np.float32).astype(BF), "yz": z.reshape(N, 128, L).astype(np.float32).astype(BF)}

@@ -1,0 +1,660 @@
+from concourse.mybir import AluOpType as ALU, ActivationFunctionType as ACT
+
+VIS = 5
+CHUNKS = [(0, 8), (8, 16)]
+CUTS = [0, 4, 8, 12, 16]
+R3 = {1, 2}
+XV = set()
+MV = {1}
+UV = set()
+ZV = set()
+NP = set()
+V3 = set()
+Y2 = set()
+YF = set()
+SEL = (0, 0)
+RS = set()
+PS = False
+XV0 = {1}
+EC = set()
+PLACE = ""
+SHIFT = ""
+INORDER = False
+ORDER = "000103020405060708090a0v0b0w0x0l0m0c0n0r0d0e0y0f0s0u14151n0g0h0W1816170i0Z191a1o0j1p1q1r1s1b1t0k0z0A0B0F1c0q0H0I0J1u0o0p0M1G0P0S0E0R0K0L0O0U0T1O0G0N0C0Q0X1e0D1d1f1v1g0Y2L1h1j1Z111H1B1i1k1C1l2a1I1D101m1w1x1J1R1y1K1S1P1z1E1U1L1Q1W1A1F2b2d1T1V1M202c0t1N1X1Y2f2i2j22250V232127262k2l2p2m2x2n2q2o24282e2r2t2s2y2z2u2w2g13122D2v2G2E2F2H292I2A2h2S2T2K2M2N2U2O2V2P2W2B2X302Y312Z38342C373l3A3B3C2J3E3s3335393O3d3D3F3e3g3G3f363P3a3h2Q3J3i3H3b3c3t3T3k3U3I3j3n3u3V3W3Q323m2R3p3R473K5h483L3Y3M3o4c3q3X3Z3N493r4k3S4a4f4n4g4d42434e404445414v4G3w464l4b4o4h4i4j4w3x4q4m4r4p4y4H4J4s4t4z4u4I4x4A4O3y4B4C4P4Q4R4T4V4S4U4W4X4Y544L4D4E3v3z504K554M514F4Z52595a5b5c5d5e53564N5o5p5g5i5j5R5q5k5m5r5v5t575s5z5w5u5C5866675n68695x5D5l5E5F5A5B5Y5y5f6k6f6a5G5H5I5J6b5X5M6c5K5L6d5N5O5Q5P6p6q6e6l6D6r6s5Z6I6m6g5S5T7N6n6h6o6T5V6E606u6i5U5W6L626t6Q6v6j6M6y6F6w6J6K6G636z6x717c6A6B6R6C6H726U6N6O6P6S6W6X6V6Y7f74647d6Z707k75777l7m7n7p7o7q7s7t7r6573797e7v78767w7x7h7a7A617B7g7i7z7F7u7H7I7b7G7J7y7T7K7j7M7C7U7V7O7W7P8n7X7Q7S7Y817Z827D7E8C8D8E808688837R8G898a858F7L8u8L8b8H878f8I8g8h8i8J8j8Q8c848d8e8V8K8k8l8m8M8v8R8W998S8N9e8t8T9m8o8p8q8U8O8r8X8Z8P8waj9h8s8Y90959a9f9b8y9p919i949c9g969j928z9q939x9I979n9s9k9d989y9J9r9o9u9t9L9A9v9l9B9w9Q9R9S9K8A9T9z9D9V9U9C9E9N9F9Xa19G9Y9W9Za0a6a79M9O8Ba2a5a39Ha4a88xabadaeacafag9PaqaraiakalaTasataxaua9aaambabbavaybcaEaCawaoapazaFanbeaGbdaHaIaDb0bfahbjaBaLbgaNaMaOaJaKbtbhboaPaQbibpb1aRbubqbkaAbraSaUaVb2bsaWbvaYbMblaXaZbmbXbHbUcQbPbnbwbybIbNbYbxbDbCbJbEbzbKbQbObFbAbGbBc5cgbLbVc6b4b5bWbRbSbTc0b9chbZc2c1cjc3b8c8c9c4cocpciclcbcac7cdb6cccqcrctcscucwcxcDckb7cvczb3cecycEcIcmcAcKcfcBcCcLcJcMcNcncVcWcXcFcPcRcYcScTdCcZdpd0cUcGd3dDd8d1dydzd4cHdudadbdEdvd2d6d5djd7cOd9dcdddedFdIdfdgdhdidldmdndJdkdodwdxdrdtdqdsdAdBdGdH"
+DELTA = {}
+NENG = 8
+MAGIC = 12582912.0
+
+F, H, I, U = "float32", "bfloat16", "int32", "uint16"
+SCRATCH = {
+    "tab": ("sbuf", [128, 4096], H), "X": ("sbuf", [128, 4096], H), "DV": ("sbuf", [128, 4096], H),
+    "DY": ("sbuf", [128, 4096], H), "AV": ("sbuf", [128, 16, 16, 16], H), "AY": ("sbuf", [128, 16, 16, 16], H),
+    "MK": ("sbuf", [128, 4096], H), "MS": ("sbuf", [128, 4096], H), "ONE": ("sbuf", [128, 2048], H),
+    "pool": ("sbuf", [128, 2048], F), "pooli": ("sbuf", [128, 1024], I), "nbi": ("sbuf", [128, 768], I),
+    "ZV0": ("sbuf", [128, 512], H), "ZV1": ("sbuf", [128, 512], H),
+    "OFF": ("sbuf", [128, 768], U), "QI": ("sbuf", [128, 768], I), "QS": ("sbuf", [128, 768], I),
+    "N32": ("sbuf", [128, 768], F), "T1": ("sbuf", [128, 256], F), "T2": ("sbuf", [128, 256], H),
+    "SG": ("sbuf", [128, 256], F), "E": ("sbuf", [128, 256], F), "FK": ("sbuf", [128, 256], F),
+    "SR": ("sbuf", [128, 16], F), "C32": ("sbuf", [128, 8], F),
+    "tab2": ("sbuf", [128, 2048], H), "pool2": ("sbuf", [128, 1024], F),
+    "DM": ("sbuf", [128, 16], I), "ic": ("sbuf", [128, 128], F), "idd": ("sbuf", [128, 128], F),
+    "K": ("sbuf", [128, 16], I), "W1": ("sbuf", [128, 32], I), "O1": ("sbuf", [128, 32], U),
+    "UM": ("sbuf", [128, 16], I), "W2": ("sbuf", [128, 64], I), "W2s": ("sbuf", [128, 64], F),
+    "O2": ("sbuf", [128, 64], U), "B2": ("sbuf", [128, 64], F),
+    "M": ("sbuf", [128, 256], H), "XI": ("sbuf", [128, 256], H), "DI": ("sbuf", [128, 256], H),
+    "D4": ("sbuf", [128, 16, 16, 16], H), "Zn2": ("sbuf", [128, 144], H), "RL": ("sbuf", [128, 512], F),
+    "I8k": ("sbuf", [128, 128], H), "In4k": ("sbuf", [128, 128], H),
+    "CUT": ("sbuf", [128, 256], H), "RT": ("sbuf", [128, 512], F), "TC": ("sbuf", [128, 1280], H),
+    "wi": ("sbuf", [128, 4], I), "di": ("sbuf", [128, 4], I), "ci": ("sbuf", [128, 8], I), "cf": ("sbuf", [128, 16], F),
+    "THR": ("sbuf", [128, 8], F), "junk": ("sbuf", [128, 16], F),
+    "iJ": ("sbuf", [128, 144], F), "iB": ("sbuf", [128, 128], F), "ia": ("sbuf", [128, 256], F),
+    "ib": ("sbuf", [128, 256], F),
+    "i16": ("sbuf", [128, 16], F), "B4": ("sbuf", [128, 16], F), "ta": ("sbuf", [128, 256], H), "tb": ("sbuf", [128, 256], H),
+    "Wb": ("sbuf", [128, 128], H), "Zp": ("sbuf", [128, 144], H), "Zn": ("sbuf", [128, 144], H), "Zw": ("sbuf", [128, 144], H),
+    "onef": ("sbuf", [128, 128], F), "If": ("sbuf", [128, 128], F), "Inf": ("sbuf", [128, 128], F),
+    "Ib": ("sbuf", [128, 128], H), "I2": ("sbuf", [128, 128], H), "Inb": ("sbuf", [128, 128], H),
+    "Ih": ("sbuf", [128, 128], H), "Cq": ("sbuf", [128, 128], H), "I32": ("sbuf", [128, 128], F),
+    "Dh": ("sbuf", [128, 128], H), "Dl": ("sbuf", [128, 128], H),
+    "Cn": ("sbuf", [128, 128], H), "oneb": ("sbuf", [128, 128], H), "zero": ("sbuf", [128, 128], H),
+    "D0": ("sbuf", [128, 136], F), "DL": ("sbuf", [128, 136], F),
+}
+for _t in range(VIS + 1):
+    SCRATCH["NB%d" % _t] = ("sbuf", [128, 1024], F)
+for _n in ("pD0", "pD1", "pU", "pA", "pB", "pF", "pR0", "pR1"):
+    SCRATCH[_n] = ("psum", [128, 512], F)
+DRAM = {"xt": H, "zt": H, "ch": I, "pa": I, "vi": I, "pl": I, "wt": I, "de": I,
+        "yc": F, "yp": F, "yq": F, "yl": F, "yx": H, "yz": H}
+SIZE = {F: 4, H: 2, I: 4, U: 2}
+
+
+def dtype(name):
+    return DRAM[name] if name in DRAM else SCRATCH[name][2]
+
+
+def R(name, lo, hi, step=1, parts=None):
+    return {"ref": name, "lo": lo, "hi": hi, "n": len(range(lo, hi, step)),
+            "ix": (slice(None) if parts is None else slice(*parts), slice(lo, hi) if step == 1 else slice(lo, hi, step))}
+
+
+def R4(name, c0, c1, r=None):
+    ix = (slice(None), slice(c0, c1)) if r is None else (slice(None), slice(c0, c1), r)
+    return {"ref": name, "lo": 256 * c0, "hi": 256 * c1, "n": (c1 - c0) * (256 if r is None else 16), "ix": ix}
+
+
+def IND(win, off):
+    return {"ref": win["ref"], "lo": win["lo"], "hi": win["hi"], "n": 16 * off["n"], "ix": win["ix"], "off": off}
+
+
+def isref(a):
+    return isinstance(a, dict)
+
+
+def psum(a):
+    return a["ref"][0] == "p" and a["ref"] in SCRATCH and SCRATCH[a["ref"]][0] == "psum"
+
+
+CY, PCY, LAT = 1.04, 0.55, 120.0
+
+
+def program():
+    ops, visit, seen = [], [-1], {}
+
+    def add(eng, kind, args, dur, **kw):
+        rd, wr = [], []
+        for call in (args if kind == "mm" else [args]):
+            for j, a in enumerate(call):
+                if isref(a):
+                    (wr if j == 0 else rd).append(a)
+                    if "off" in a:
+                        rd.append(a["off"])
+        if kw.get("accum") is not None:
+            wr.append(kw["accum"])
+        op = {"eng": eng, "kind": kind, "args": args, "dur": dur, "rd": rd, "wr": wr}
+        op.update(kw)
+        name = wr[0]["ref"]
+        name = name[:2] if name[:2] in ("NB", "ZV", "pR") else name
+        base = "%s%s%s%d" % ("" if visit[0] >= 0 else "s", eng, name, 0 if name == "THR" else wr[0]["lo"])
+        seen[(visit[0], base)] = seen.get((visit[0], base), 0) + 1
+        op["tag"] = "%s.%d" % (base, seen[(visit[0], base)])
+        op["visit"] = visit[0]
+        ops.append(op)
+        return op
+
+    def cost(out, ins, two=False):
+        if "off" in out:
+            return 50 + 3.8 * CY * out["n"]
+        if "off" in ins[0]:
+            return 55 + 1.56 * CY * ins[0]["n"]
+        f = 0.5 if all(SIZE[dtype(a["ref"])] == 2 for a in [out] + ins) else 1.0
+        if two:
+            f = 1.0 if any(psum(a) for a in ins) else 2.0
+        return 30 + CY * max(64, f * out["n"])
+
+    def cp(out, a):
+        add("V", "cp", [out, a], cost(out, [a]))
+
+    def tt(out, a, b, op):
+        add("V", "tt", [out, a, b, op], cost(out, [a, b], True))
+
+    def ts(out, a, s1, op0, s2=None, op1=None):
+        add("V", "ts", [out, a, s1, s2, op0, op1], cost(out, [a]))
+
+    def scan(out, a, b, op0, op1):
+        add("V", "scan", [out, a, b, op0, op1], cost(out, [a, b]))
+
+    def ms(out, v):
+        add("V", "ms", [out, v], cost(out, [out]))
+
+    def act(out, a, fn, bias=0.0, scale=1.0, accum=None):
+        d = 65 + 1.56 * CY * a["n"] if "off" in a else 40 + CY * max(64, a["n"])
+        add("S", "act", [out, a, fn, bias, scale], d, accum=accum)
+
+    def mm(calls, **kw):
+        d = 40 + sum(max(64, c[0]["n"]) * (4 if dtype(c[1]["ref"]) == F else 1) * PCY for c in calls)
+        add("P", "mm", calls, d, **kw)
+
+    def group(out, pairs, start=True, stop=True):
+        return [[out, a, b, start and j == 0, stop and j == len(pairs) - 1] for j, (a, b) in enumerate(pairs)]
+
+    def iota(out, pattern, base, cm):
+        add("G", "iota", [out, pattern, base, cm], 140 + 2 * CY * out["n"])
+
+    def dma(q, out, a):
+        add(q, "dma", [out, a], 60, bytes=128 * out["n"] * SIZE[dtype(out["ref"])])
+
+    def gather(eng, out, src):
+        if eng == "V":
+            cp(out, src)
+        else:
+            act(out, src, ACT.Copy)
+
+    col = lambda j: R("cf", j, j + 1)
+    G16, KF, C16, C4, CN, WF = (col(j) for j in range(6))
+    M128 = lambda name: R(name, 0, 128)
+    lanes = [(16 * a, 16 * b) for a, b in CHUNKS]
+
+    def zv(t, x, part):
+        l0, l1 = lanes[x]
+        n = l1 - l0
+        return R("ZV%d" % (t % 2), 2 * l0 + part * n, 2 * l0 + (part + 1) * n)
+
+    def nb(t, s, x):
+        return R("NB%d" % t, 256 * s + lanes[x][0], 256 * s + lanes[x][1])
+
+    dma("Y", R("wi", 0, 1), R("wt", 0, 1))
+    for x, (l0, l1) in enumerate(lanes):
+        dma("S", zv(0, x, 0), R("zt", l0, l1))
+    dma("Y", R("nbi", 256, 512), R("ch", 0, 256))
+    dma("Y", R("tab", 0, 2048), R("xt", 0, 2048))
+    dma("S", R("tab", 2048, 4096), R("xt", 2048, 4096))
+    dma("Y", R("nbi", 512, 768), R("vi", 0, 256))
+    dma("Y", R("nbi", 0, 256), R("pa", 0, 256))
+    dma("Y", R("di", 0, 1), R("de", 0, 1))
+    dma("Y", R("pooli", 0, 1024), R("pl", 0, 1024))
+    iota(R("ci", 0, 1), [[0, 1]], 0, 1)
+    iota(M128("iB"), [[16, 8], [0, 16]], 0, 0)
+    iota(M128("onef"), [[0, 128]], 1, 0)
+    add("G", "sel", [M128("If"), M128("onef")], 170 + 2 * CY * 128)
+    iota(R("iJ", 0, 144), [[1, 144]], -15, 0)
+    iota(M128("ic"), [[-3840, 8], [1, 16]], 28672, 0)
+    iota(M128("idd"), [[32, 8], [0, 16]], 1, 0)
+    iota(R("i16", 0, 8), [[256, 8]], 0, 0)
+    iota(R("ia", 0, 256), [[0, 16], [1, 16]], 0, 0)
+    iota(R("ib", 0, 256), [[-1, 16], [0, 16]], 15, 0)
+    iota(R("ONE", 0, 2048), [[0, 2048]], 1, 0)
+    ts(R("ci", 1, 2), R("ci", 0, 1), 112, ALU.bitwise_and)
+    ts(R("ci", 2, 3), R("ci", 0, 1), 15, ALU.bitwise_and)
+    cp(G16, R("ci", 1, 2))
+    cp(KF, R("ci", 2, 3))
+    ts(C16, R("ci", 2, 3), 16.0, ALU.mult)
+    ts(C4, R("ci", 2, 3), 4.0, ALU.mult)
+    ts(CN, R("ci", 2, 3), 1184.0, ALU.mult, -262144.0, ALU.add)
+    cp(WF, R("wi", 0, 1))
+    ts(R("THR", 0, 1), R("di", 0, 1), 1.0 - 1.0 / 65536, ALU.add)
+    if RS:
+        iota(R("C32", 0, 8), [[-32, 8]], 0, 0)
+    ts(M128("Wb"), M128("iB"), G16, ALU.is_equal, WF, ALU.mult)
+    ms(R("Cn", 0, 128, parts=(0, 32)), -64.0)
+    ms(R("Cn", 0, 128, parts=(32, 64)), 1.0 / 64)
+    ms(M128("oneb"), 1.0)
+    act(M128("Ib"), M128("If"), ACT.Copy)
+    act(M128("Inf"), M128("If"), ACT.Copy, scale=-1.0)
+    act(M128("Inb"), M128("If"), ACT.Copy, scale=-1.0)
+    if len(ZV) < 2:
+        act(M128("I2"), M128("If"), ACT.Copy, scale=2.0)
+    if any(SEL):
+        act(M128("I8k"), M128("If"), ACT.Copy, scale=8192.0)
+        act(M128("In4k"), M128("If"), ACT.Copy, scale=-4096.0)
+    if Y2:
+        ts(R("Zn2", 0, 144), R("iJ", 0, 144), G16, ALU.is_equal, -2.0, ALU.mult)
+    if ZV:
+        act(M128("Ih"), M128("If"), ACT.Copy, scale=0.5)
+        ms(R("Cq", 0, 128, parts=(0, 64)), -1.0 / 256)
+    if NP:
+        ts(col(6), R("ci", 2, 3), 1024.0, ALU.mult, -262144.0, ALU.add)
+        ts(col(7), R("ci", 2, 3), 160.0, ALU.mult)
+        act(M128("I32"), M128("If"), ACT.Copy, scale=32.0)
+        act(M128("Dh"), M128("If"), ACT.Copy, scale=col(6))
+        act(M128("Dl"), M128("If"), ACT.Copy, scale=col(7))
+    ts(R("Zp", 0, 144), R("iJ", 0, 144), G16, ALU.is_equal)
+    ts(R("Zn", 0, 144), R("iJ", 0, 144), G16, ALU.is_equal, -1.0, ALU.mult)
+    ts(R("Zw", 0, 144), R("iJ", 0, 144), G16, ALU.is_equal, WF, ALU.mult)
+    act(M128("ic"), M128("ic"), ACT.Copy, scale=1.0 / 32768)
+    tt(M128("D0"), M128("ic"), M128("idd"), ALU.add)
+    ms(M128("DL"), 16.0 / 32768)
+    ts(col(9), R("ci", 2, 3), 16.0, ALU.mult, 1807.0, ALU.add)
+    ms(M128("zero"), 0.0)
+    ts(R("B4", 0, 8), R("i16", 0, 8), 0.25, ALU.mult, C4, ALU.add)
+    for c0, c1 in CHUNKS:
+        C = c1 - c0
+        ts(R("B2", 4 * c0, 4 * c0 + C), R("i16", 0, C), C16, ALU.add)
+        ms(R("B2", 4 * c0 + C, 4 * c0 + 2 * C), 0.0)
+        dma("Y", R("MK", 256 * c0, 256 * c1), R("ONE", 0, 256 * C))
+    ms(R("TC", 0, 512), 0.0)
+    ms(R("TC", 768, 1280), 0.0)
+    ts(R("ta", 0, 256), R("ia", 0, 256), KF, ALU.is_le)
+    ts(R("tb", 0, 256), R("ib", 0, 256), KF, ALU.is_ge)
+    tt(R("TC", 512, 768), R("ta", 0, 256), R("tb", 0, 256), ALU.mult)
+    for x, (l0, l1) in enumerate(lanes):
+        for s in (1, 2, 0):
+            cp(nb(0, s, x), R("nbi", 256 * s + l0, 256 * s + l1))
+    for j in range(2):
+        cp(R("pool", 512 * j + 512, 512 * j + 1024), R("pooli", 512 * j, 512 * j + 512))
+
+    TAB = R("tab", 0, 4096)
+    sel = lambda name, r: R(name, 15 - r, 143 - r)
+    nr3 = [0]
+    for t in range(VIS):
+        last = t == VIS - 1
+        visit[0] = t
+        if last:
+            dma("Y", R("tab2", 0, 2048), R("tab", 0, 2048))
+            dma("Y", R("pool2", 512, 1024), R("pool", 512, 1024))
+        for x, (l0, l1) in enumerate(lanes):
+            n = l1 - l0
+            bank = ("pA", "pB")[x % 2]
+            z = zv(t, x, 0)
+            mm(group(R("pU", 0, n), [(M128("Wb"), z), (R("Cn", 0, 128, parts=(0, 64)), R("oneb", 0, n, parts=(0, 64)))]))
+            if x in UV:
+                ts(R("T2", l0, l1), R("pU", 0, n), 4096 * MAGIC, ALU.add, 4096 * MAGIC, ALU.subtract)
+                mm(group(R(bank, 0, n), [(M128("Wb"), z), (M128("Inb"), R("T2", l0, l1))]))
+            else:
+                act(R("T1", l0, l1), R("pU", 0, n), ACT.Identity, MAGIC, 1.0 / 4096)
+                act(R("T2", l0, l1), R("T1", l0, l1), ACT.Identity, 4096 * MAGIC, -4096.0)
+                mm(group(R(bank, 0, n), [(M128("Wb"), z), (M128("Ib"), R("T2", l0, l1))]))
+            for s in (1, 2, 0):
+                a, b = 256 * s + l0, 256 * s + l1
+                P, N = R(bank, 128 * (s + 1), 128 * (s + 1) + n), R("N32", a, b)
+                if 3 * x + s in NP:
+                    P, N = N, P
+                    mm(group(N, [(M128("I32"), nb(t, s, x)), (M128("Dh"), R("oneb", 0, n)), (M128("Dl"), R("oneb", 0, n))]))
+                else:
+                    act(N, nb(t, s, x), ACT.Identity, CN, 32.0)
+                tt(P, nb(t, s, x), R(bank, 0, n), ALU.mult)
+                tt(R("QI", a, b), P, N, ALU.add)
+                ts(R("QS", a, b), R("QI", a, b), 5, ALU.arith_shift_right, 4095, ALU.bitwise_and)
+                cp(R("OFF", a, b), R("QS", a, b))
+        for pc, (a, b) in enumerate(zip(CUTS[:-1], CUTS[1:])):
+            if True:
+                big = lambda name, u=a, v=b: R(name, 256 * u, 256 * v)
+                off = lambda s: R("OFF", 256 * s + 16 * a, 256 * s + 16 * b)
+                bank = ("pD0", "pD1")[pc % 2]
+                whole = R(bank, 0, 512)
+                D = R(bank, 0, 16 * (b - a))
+                gather("V" if pc in (XV if t else XV0) else "S", big("X"), IND(TAB, off(1)))
+                sums = []
+                for s, dn, an, zn, by_s in ((2, "DV", "AV", "Zp", a // 8 in V3), (0, "DY", "AY", "Zn", pc in R3)):
+                    pairs = [(sel(zn, r), R4(an, a, b, r)) for r in range(16)]
+                    if by_s:
+                        gather("S", big(dn), IND(TAB, off(s)))
+                        for u in range(a, b, 2):
+                            v = min(u + 2, b)
+                            pr = R(("pR0", "pR1")[nr3[0] % 2], 0, 256 * (v - u))
+                            nr3[0] += 1
+                            mm(group(pr, [(M128("Ib"), big(dn, u, v)), (M128("Inb"), big("X", u, v))]))
+                            act(R4(an, u, v), pr, ACT.Abs)
+                    elif s == 0 and pc in Y2:
+                        tt(R4("D4", a, b), IND(TAB, off(s)), big("X"), ALU.subtract)
+                        ts(R4(an, a, b), R4("D4", a, b), 0.0, ALU.max)
+                        pairs = ([(sel("Zp", r), R4("D4", a, b, r)) for r in range(16)]
+                                 + [(sel("Zn2", r), R4(an, a, b, r)) for r in range(16)])
+                    else:
+                        tt(big(dn), IND(TAB, off(s)), big("X"), ALU.subtract)
+                        act(R4(an, a, b), big(dn), ACT.Abs)
+                    sums.append(pairs)
+                if pc in YF:
+                    sums.reverse()
+                for j, pairs in enumerate(sums):
+                    mm(group(D, pairs, j == 0, j == 1))
+                    ops[-1]["wr"].append(whole)
+                act(R("SG", 16 * a, 16 * b), D, ACT.Sign, scale=-1.0)
+        for x, (c0, c1) in enumerate(CHUNKS):
+            C = c1 - c0
+            l0, l1 = lanes[x]
+            n = l1 - l0
+            ln = lambda name: R(name, l0, l1)
+            sm = lambda name, w=1, p0=0, p1=None: R(name, w * c0 + p0 * C, w * c0 + (w if p1 is None else p1) * C)
+            big = lambda name: R(name, 256 * c0, 256 * c1)
+            K = sm("K")
+            oi, oj = sm("O1", 2, 0, 1), sm("O1", 2, 1, 2)
+            scan(ln("E"), R("D0", 0, n), ln("SG"), ALU.max, ALU.add)
+            scan(ln("FK"), R("DL", 0, n), ln("E"), ALU.add, ALU.max)
+            ts(K, R("FK", l0 + 15, l1, 16), 32768.0, ALU.mult)
+            ts(sm("W1", 2, 0, 1), K, 0x70F, ALU.bitwise_and)
+            ts(oi, sm("W1", 2, 0, 1), C16, ALU.add)
+            ts(sm("W1", 2, 1, 2), K, 4, ALU.logical_shift_right, 0x70F, ALU.bitwise_and)
+            ts(oj, sm("W1", 2, 1, 2), -1.0, ALU.mult, col(9), ALU.add)
+            if x not in RS:
+                ts(sm("DM"), K, 15, ALU.logical_shift_right, 31, ALU.bitwise_and)
+            cp(IND(big("MK"), oi), R("zero", 0, n))
+            scan(big("MS"), big("MK"), big("X"), ALU.mult, ALU.max)
+            if not last:
+                dma("Y", big("MK"), R("ONE", 0, 256 * C))
+            ts(sm("W2", 4, 3, 4), K, 255, ALU.bitwise_and)
+            if x in RS:
+                g1, g2 = R("pU", 160 + c0, 160 + c1), R("pU", 176 + c0, 176 + c1)
+                mm(group(g1, [(M128("If"), R("FK", l0 + 15, l1, 16)), (M128("If"), R("C32", 0, C))]))
+                act(sm("SR"), g1, ACT.Sign, R("THR", t, t + 1), -1.0)
+                act(sm("B2", 4, 3, 4), sm("SR"), ACT.Identity, 256.0, (-256.0, 256.0)[x])
+                mm(group(g2, [(M128("If"), sm("B2", 4, 3, 4)), (M128("If"), R("B4", 0, C))]))
+                act(sm("B2", 4, 2, 3), g2, ACT.Copy)
+            else:
+                ts(sm("B2", 4, 3, 4), sm("DM"), R("THR", t, t + 1), (ALU.is_ge, ALU.is_lt)[x], 512.0, ALU.mult)
+                tt(sm("B2", 4, 2, 3), sm("B2", 4, 3, 4), R("B4", 0, C), ALU.add)
+            gather("S", ln("XI"), IND(big("X"), oi))
+            gather("S", ln("DI"), IND(big("DV"), oi))
+            gather("V" if x in MV else "S", ln("M"), IND(big("MS"), oj))
+            um = R("pU", 128 + c0, 128 + c1)
+            mm(group(um, [(sel("Zw", r), R("M", l0 + r, l1, 16)) for r in range(16)]))
+            znew = R("ZV%d" % ((t + 1) % 2), 2 * l0, 2 * l1)
+            if x in ZV:
+                q4 = (R("Cq", 0, 128, parts=(0, 64)), R("oneb", 0, n, parts=(0, 64)))
+                mm(group(R("pF", 256 + n, 256 + 2 * n), [q4, (M128("Ih" if x in V3 else "Ib"), ln("XI")), (M128("Ih"), ln("DI"))])
+                   + group(R("pF", 256, 256 + n), [q4, (M128("Ih"), zv(t, x, 0)), (M128("Ih"), ln("M"))]))
+                ts(znew, R("pF", 256, 256 + 2 * n), MAGIC, ALU.add, MAGIC, ALU.subtract)
+            else:
+                mm(group(R("pF", 256 + n, 256 + 2 * n), [(M128("Ib" if x in V3 else "I2"), ln("XI")), (M128("Ib"), ln("DI"))])
+                   + group(R("pF", 256, 256 + n), [(M128("Ib"), zv(t, x, 0)), (M128("Ib"), ln("M"))]))
+                rt = R("RT", 2 * l0, 2 * l1)
+                act(rt, R("pF", 256, 256 + 2 * n), ACT.Identity, MAGIC, 0.4999)
+                act(znew, rt, ACT.Identity, -MAGIC)
+            cp(sm("UM"), um)
+            for j, bits in enumerate((15, 1023, 3)):
+                ts(sm("W2", 4, j, j + 1), sm("UM"), bits, ALU.bitwise_and)
+            for p0, p1 in (((3, 4), (0, 3)) if x in EC or last and x == 1 else ((0, 4),)):
+                tt(sm("W2s", 4, p0, p1), sm("W2", 4, p0, p1), sm("B2", 4, p0, p1), ALU.add)
+                cp(sm("O2", 4, p0, p1), sm("W2s", 4, p0, p1))
+            gather("S", nb(t + 1, 0, x), IND(R("pool", 512, 1536), sm("O2", 4, 1, 2)))
+            gather("S", ln("CUT"), IND(R("TC", 512 * x, 512 * x + 768), sm("O2", 4, 3, 4)))
+            d1, d2 = R("pU", 256, 256 + n), R("pU", 384, 384 + n)
+            e1, e2 = R("pF", 0, n), R("pF", 128, 128 + n)
+            up = [(M128("I8k"), ln("CUT"))] if SEL[x] else []
+            mm(group(d1, [(M128("If"), nb(t, 0, x)), (M128("Inf"), nb(t, 1, x))] + up)
+               + group(d2, [(M128("If"), nb(t, 1, x)), (M128("Inf"), nb(t, 2, x))] + up))
+            if SEL[x] == 0:
+                tt(e2, d2, ln("CUT"), ALU.mult)
+                tt(e1, d1, ln("CUT"), ALU.mult)
+                tt(nb(t + 1, 3, x), e2, nb(t, 2, x), ALU.add)
+                tt(nb(t + 1, 1, x), e1, nb(t, 1, x), ALU.add)
+            else:
+                r1, r2 = R("RL", 2 * l0, 2 * l0 + n), R("RL", 2 * l0 + n, 2 * l1)
+                act(R("RL", 2 * l0, 2 * l1), R("pU", 256, 512), ACT.Relu, -4096.0)
+                down = (M128("In4k"), ln("CUT"))
+                if SEL[x] == 1:
+                    mm(group(e1, [(M128("If"), nb(t, 1, x)), down]) + group(e2, [(M128("If"), nb(t, 2, x)), down]))
+                    tt(nb(t + 1, 3, x), e2, r2, ALU.add)
+                    tt(nb(t + 1, 1, x), e1, r1, ALU.add)
+                else:
+                    mm(group(e1, [(M128("If"), nb(t, 1, x)), down, (M128("If"), r1)])
+                       + group(e2, [(M128("If"), nb(t, 2, x)), down, (M128("If"), r2)]))
+                    act(nb(t + 1, 1, x), e1, ACT.Copy)
+                    act(nb(t + 1, 3, x), e2, ACT.Copy)
+            if not last:
+                add("G", "send", [nb(t + 1, 2, x), nb(t + 1, 3, x)], 1000, bytes=128 * n * 4)
+                mm(group(R("pU", 144 + c0, 144 + c1), [(M128("onef"), sm("B2", 4, 3, 4))]))
+        for x, (c0, c1) in enumerate(CHUNKS):
+            C = c1 - c0
+            tab = R("tab2" if last and x == 0 else "tab", 256 * c0, 256 * c1)
+            cp(IND(tab, R("O2", 4 * c0, 4 * c0 + C)), zv(t + 1, x, 1))
+            if last:
+                dma("Y", R("yx", 256 * c0, 256 * c1), tab)
+        for x, (c0, c1) in enumerate(CHUNKS):
+            C = c1 - c0
+            pool = "pool2" if last and x == 0 else "pool"
+            cp(IND(R(pool, 1024 * x, 1024 * x + 1024), R("O2", 4 * c0 + 2 * C, 4 * c0 + 3 * C)), nb(t + 1, 1, x))
+            if last:
+                dma("Y", R("yl", 512 * x, 512 * x + 512), R(pool, 512 * x + 512, 512 * x + 1024))
+        if not last:
+            act(R("junk", 0, 16), R("pU", 144, 160), ACT.Copy, scale=1.0 / 512, accum=col(8))
+            if PS:
+                act(col(10), col(8), ACT.Identity, MAGIC, 0.4999)
+                act(col(11), col(10), ACT.Identity, 2 * MAGIC, -2.0)
+                act(col(12), col(8), ACT.Identity, col(11))
+                act(R("THR", t + 1, t + 2), col(12), ACT.Identity, R("THR", 0, 1))
+            else:
+                cp(R("ci", 4, 5), col(8))
+                ts(R("ci", 5, 6), R("ci", 4, 5), 1, ALU.bitwise_and)
+                ts(R("THR", t + 1, t + 2), R("ci", 5, 6), R("THR", 0, 1), ALU.add)
+    for x, (l0, l1) in enumerate(lanes):
+        q = "S" if x == len(lanes) - 1 else "Y"
+        dma(q, R("yq", l0, l1), nb(VIS, 3, x))
+        dma(q, R("yc", l0, l1), nb(VIS, 1, x))
+        dma(q, R("yz", l0, l1), zv(VIS, x, 0))
+        dma(q, R("yp", l0, l1), nb(VIS, 0, x))
+    return ops
+
+
+def depend(ops):
+    hist = {}
+    for j, op in enumerate(ops):
+        pre, raw = set(), set()
+        for a, w in [(a, False) for a in op["rd"]] + [(a, True) for a in op["wr"]]:
+            for (lo, hi, k, kw) in hist.get(a["ref"], []):
+                if (w or kw) and lo < a["hi"] and a["lo"] < hi and k != j:
+                    pre.add(k)
+                    if kw and not w:
+                        raw.add(k)
+        for a in op["wr"]:
+            hist[a["ref"]] = [e for e in hist.get(a["ref"], []) if not (a["lo"] <= e[0] and e[1] <= a["hi"] and e[2] != j)]
+        for a, w in [(a, False) for a in op["rd"]] + [(a, True) for a in op["wr"]]:
+            hist.setdefault(a["ref"], []).append((a["lo"], a["hi"], j, w))
+        op["pre"] = pre
+        op["own"] = {k for k in pre - raw if INORDER and ops[k]["eng"] == op["eng"] and "bytes" not in ops[k] and "bytes" not in op
+                     and not any("off" in a for a in op["wr"] + ops[k]["wr"])}
+        op["banks"] = {a["ref"] for a in op["rd"] + op["wr"] if psum(a)}
+
+
+def flight(op):
+    return 0.0 if "bytes" not in op else 1900.0 + op["bytes"] / 220.0
+
+
+def schedule(ops, delta):
+    n = len(ops)
+    suc = [[] for _ in ops]
+    for j, op in enumerate(ops):
+        for k in op["pre"]:
+            suc[k].append(j)
+    prio = [0.0] * n
+    for j in range(n - 1, -1, -1):
+        prio[j] = ops[j]["dur"] + flight(ops[j]) + max([LAT + prio[k] for k in suc[j]] + [0.0])
+    prio = [p + delta.get(op["tag"], 0) for p, op in zip(prio, ops)]
+    left = [len(op["pre"]) for op in ops]
+    rdy = {e: [] for e in "VSPGY"}
+    at = [0.0] * n
+    for j in range(n):
+        if left[j] == 0:
+            rdy[ops[j]["eng"]].append(j)
+    free = {e: 0.0 for e in rdy}
+    bank, order, extra, fin, wire = {}, [], {}, [0.0] * n, [0.0]
+
+    def est(j):
+        s = max(at[j], free[ops[j]["eng"]])
+        for b in ops[j]["banks"]:
+            for e, k in bank.get(b, {}).items():
+                if e != ops[j]["eng"]:
+                    s = max(s, fin[k] + LAT)
+        return s
+
+    while len(order) < n:
+        best = None
+        for e, lst in rdy.items():
+            if not lst:
+                continue
+            es = {j: est(j) for j in lst}
+            t0 = min(es.values())
+            pick = None
+            for c in lst:
+                end = es[c] + ops[c]["dur"]
+                score = max([es[c] + prio[c]] + [max(es[o], end) + prio[o] for o in lst if o != c]) + IDLE * (es[c] - t0)
+                key = (score, -prio[c])
+                if pick is None or key < pick[0]:
+                    pick = (key, c)
+            c = pick[1]
+            if best is None or es[c] < best[0]:
+                best = (es[c], c)
+        s, j = best
+        op = ops[j]
+        e = op["eng"]
+        rdy[e].remove(j)
+        extra[j] = set()
+        for b in op["banks"]:
+            extra[j] |= {k for f, k in bank.get(b, {}).items() if f != e}
+            bank.setdefault(b, {})[e] = j
+        free[e] = s + op["dur"]
+        fin[j] = free[e]
+        if "bytes" in op:
+            wire[0] = max(wire[0], fin[j] + 1900.0) + op["bytes"] / 220.0
+            fin[j] = wire[0]
+        order.append(j)
+        for k in suc[j]:
+            at[k] = max(at[k], fin[j] + LAT)
+            left[k] -= 1
+            if left[k] == 0:
+                rdy[ops[k]["eng"]].append(k)
+    return order, extra, max(fin)
+
+
+IDLE = 1.0
+
+
+def placed(ops):
+    place = dict(zip(sorted({op["tag"] for op in ops}), (int(v) for v in PLACE.split(","))))
+    shift = {s.split(":")[0]: int(s.split(":")[1]) for s in SHIFT.split(",") if s}
+    key = []
+    for op in ops:
+        k = 1000 * max(op["visit"], 0) + place[op["tag"]] + shift.get("%s@%d" % (op["tag"], op["visit"]), 0)
+        for p in sorted(op["pre"]):
+            if key[p] >= k:
+                k = key[p] + 0.001
+        key.append(k)
+    order = sorted(range(len(ops)), key=lambda j: (key[j], j))
+    return banks(ops, order)
+
+
+def listed(ops):
+    digits = "0123456789abcdefghijklmnopqrstuvwxyzABCDEFGHIJKLMNOPQRSTUVWXYZ"
+    order = [62 * digits.index(ORDER[i]) + digits.index(ORDER[i + 1]) for i in range(0, len(ORDER), 2)]
+    return banks(ops, order)
+
+
+def banks(ops, order):
+    bank, extra = {}, {}
+    for j in order:
+        extra[j] = set()
+        for b in ops[j]["banks"]:
+            extra[j] |= {k for f, k in bank.get(b, {}).items() if f != ops[j]["eng"]}
+            bank.setdefault(b, {})[ops[j]["eng"]] = j
+    return order, extra, 0.0
+
+
+def plan():
+    ops = program()
+    depend(ops)
+    order, extra, end = listed(ops) if ORDER else placed(ops) if PLACE else schedule(ops, DELTA)
+    count, names, known = {}, [], {e: {} for e in "VSPGY"}
+    for j in order:
+        op = ops[j]
+        e = op["eng"]
+        waits = {}
+        for k in sorted((op["pre"] - op["own"]) | extra[j], key=lambda k: -ops[k]["pos"]):
+            sem, val = ops[k]["sig"]
+            if known[e].get(sem, 0) < val and not (e == "P" and sem == "cP"):
+                waits[sem] = max(waits.get(sem, 0), val)
+                known[e][sem] = val
+                for s, v in ops[k]["knows"].items():
+                    known[e][s] = max(known[e].get(s, 0), v)
+        op["waits"] = waits
+        op["pos"] = len(names) + sum(count.values())
+        op["knows"] = {} if op["kind"] == "send" else dict(known[e])
+        if "bytes" in op:
+            names.append("d%d" % len(names))
+            op["sig"] = (names[-1], NENG if op["kind"] == "send" else 16)
+        else:
+            count[e] = count.get(e, 0) + 1
+            op["sig"] = ("c" + e, count[e])
+    return [ops[j] for j in order], names, end
+
+
+OPS, _names, ESTIMATE = plan()
+SEMAPHORES = ["cV", "cS", "cP", "cG", "sent"] + _names
+
+
+def rank_program(g, core, T, topo):
+    rank = T.rank_of(core)
+    if rank is None:
+        return
+    nxt = T.cores[(rank + 1) % len(T.cores)]
+    rid, pid = topo.addr(nxt)[:2]
+    mask = sum(1 << e for e in topo.engines(core, nxt)[:NENG])
+    Q = {"V": g.vector, "S": g.scalar, "P": g.tensor, "G": g, "Y": g.sync}
+
+    def ap(a):
+        if not isref(a):
+            return a
+        v = T[a["ref"]][a["ix"]]
+        return v.indirect(ap(a["off"])) if "off" in a else v
+
+    final, sent = {}, 0
+    for op in OPS:
+        q, kind = Q[op["eng"]], op["kind"]
+        for sem, val in op["waits"].items():
+            q.wait_ge(T.sem[sem], val)
+        sem, val = op["sig"]
+        final[sem] = val
+        if kind == "mm":
+            for c in op["args"]:
+                ins = q.matmul(ap(c[0]), ap(c[1]), ap(c[2]), c[3], c[4])
+            ins.then_inc(T.sem[sem], 1)
+            continue
+        a = [ap(v) for v in op["args"]]
+        if kind == "send":
+            g.remote_dma(a[0], a[1], T.sem[sem], T.sem.sent, pid, rid, mask)
+            sent += NENG
+            continue
+        if kind == "dma":
+            whole = [T[v["ref"]][:] if v["ref"] in ("wt", "de") else w for v, w in zip(op["args"], a)]
+            q.dma_start(whole[0], whole[1]).then_inc(T.sem[sem], 16)
+            continue
+        if kind == "cp":
+            ins = q.tensor_copy(a[0], a[1])
+        elif kind == "tt":
+            ins = q.tensor_tensor(a[0], a[1], a[2], a[3])
+        elif kind == "ts":
+            ins = q.tensor_scalar(*a[:5]) if a[5] is None else q.tensor_scalar(*a)
+        elif kind == "scan":
+            ins = q.tensor_tensor_scan(a[0], a[1], a[2], -1.0, a[3], a[4])
+        elif kind == "ms":
+            ins = q.memset(a[0], a[1])
+        elif kind == "act":
+            ins = q.activation(a[0], a[1], a[2], bias=a[3], scale=a[4], accum_out=ap(op["accum"]))
+        elif kind == "iota":
+            if dtype(op["args"][0]["ref"]) == I:
+                ins = g.iota(a[0], a[1], a[2], a[3])
+            else:
+                ins = g.iota(a[0], a[1], a[2], a[3], allow_small_or_imprecise_dtypes=True)
+        else:
+            ins = g.affine_select(a[0], a[1], [[-1, 128]], ALU.is_equal, 0.0, 0, 1)
+        ins.then_inc(T.sem[sem], 1)
+    g.wait_ge(T.sem.sent, sent)
+    for sem, val in final.items():
+        g.wait_ge(T.sem[sem], val)

@@ -1,66 +1,68 @@
+from concourse.bass import DstId, RemoteDMATransfer
 from concourse.mybir import AluOpType as ALU, ActivationFunctionType as ACT
 
 VIS = 5
-CHUNKS = [(0, 8), (8, 16)]
-CUTS = [0, 4, 8, 12, 16]
-R3 = {1, 2}
-XV = set()
-MV = {1}
-UV = set()
-ZV = set()
-NP = set()
-V3 = set()
-Y2 = set()
-YF = set()
-SEL = (0, 0)
-RS = set()
-PS = False
-XV0 = {1}
-EC = set()
-PLACE = ""
-SHIFT = ""
-INORDER = False
-ORDER = "000103020405060708090a0v0b0w0x0l0m0c0n0r0d0e0y0f0s0u14151n0g0h0W1816170i0Z191a1o0j1p1q1r1s1b1t0k0z0A0B0F1c0q0H0I0J1u0o0p0M1G0P0S0E0R0K0L0O0U0T1O0G0N0C0Q0X1e0D1d1f1v1g0Y2L1h1j1Z111H1B1i1k1C1l2a1I1D101m1w1x1J1R1y1K1S1P1z1E1U1L1Q1W1A1F2b2d1T1V1M202c0t1N1X1Y2f2i2j22250V232127262k2l2p2m2x2n2q2o24282e2r2t2s2y2z2u2w2g13122D2v2G2E2F2H292I2A2h2S2T2K2M2N2U2O2V2P2W2B2X302Y312Z38342C373l3A3B3C2J3E3s3335393O3d3D3F3e3g3G3f363P3a3h2Q3J3i3H3b3c3t3T3k3U3I3j3n3u3V3W3Q323m2R3p3R473K5h483L3Y3M3o4c3q3X3Z3N493r4k3S4a4f4n4g4d42434e404445414v4G3w464l4b4o4h4i4j4w3x4q4m4r4p4y4H4J4s4t4z4u4I4x4A4O3y4B4C4P4Q4R4T4V4S4U4W4X4Y544L4D4E3v3z504K554M514F4Z52595a5b5c5d5e53564N5o5p5g5i5j5R5q5k5m5r5v5t575s5z5w5u5C5866675n68695x5D5l5E5F5A5B5Y5y5f6k6f6a5G5H5I5J6b5X5M6c5K5L6d5N5O5Q5P6p6q6e6l6D6r6s5Z6I6m6g5S5T7N6n6h6o6T5V6E606u6i5U5W6L626t6Q6v6j6M6y6F6w6J6K6G636z6x717c6A6B6R6C6H726U6N6O6P6S6W6X6V6Y7f74647d6Z707k75777l7m7n7p7o7q7s7t7r6573797e7v78767w7x7h7a7A617B7g7i7z7F7u7H7I7b7G7J7y7T7K7j7M7C7U7V7O7W7P8n7X7Q7S7Y817Z827D7E8C8D8E808688837R8G898a858F7L8u8L8b8H878f8I8g8h8i8J8j8Q8c848d8e8V8K8k8l8m8M8v8R8W998S8N9e8t8T9m8o8p8q8U8O8r8X8Z8P8waj9h8s8Y90959a9f9b8y9p919i949c9g969j928z9q939x9I979n9s9k9d989y9J9r9o9u9t9L9A9v9l9B9w9Q9R9S9K8A9T9z9D9V9U9C9E9N9F9Xa19G9Y9W9Za0a6a79M9O8Ba2a5a39Ha4a88xabadaeacafag9PaqaraiakalaTasataxaua9aaambabbavaybcaEaCawaoapazaFanbeaGbdaHaIaDb0bfahbjaBaLbgaNaMaOaJaKbtbhboaPaQbibpb1aRbubqbkaAbraSaUaVb2bsaWbvaYbMblaXaZbmbXbHbUcQbPbnbwbybIbNbYbxbDbCbJbEbzbKbQbObFbAbGbBc5cgbLbVc6b4b5bWbRbSbTc0b9chbZc2c1cjc3b8c8c9c4cocpciclcbcac7cdb6cccqcrctcscucwcxcDckb7cvczb3cecycEcIcmcAcKcfcBcCcLcJcMcNcncVcWcXcFcPcRcYcScTdCcZdpd0cUcGd3dDd8d1dydzd4cHdudadbdEdvd2d6d5djd7cOd9dcdddedFdIdfdgdhdidldmdndJdkdodwdxdrdtdqdsdAdBdGdH"
-DELTA = {}
-NENG = 8
 MAGIC = 12582912.0
+NENG = 8
+
+PLAN = {
+    "chunks": [(0, 8), (8, 16)],
+    "pieces": [(0, 4), (4, 8), (8, 12), (12, 16)],
+    "x": "SSSS",
+    "x0": "SSSS",
+    "v": "VVGV",
+    "y": "MSFS",
+    "m": "SS",
+    "u": "SV",
+    "z": "SSSV",
+    "parity": "S",
+    "split": 1,
+    "t": "JJJJJJ",
+    "add": "SV",
+    "early": "01",
+    "apart": "01",
+    "cut": "10",
+    "pair": True,
+    "whole": "10",
+    "hbank": ["pH0"] * 3 + ["pH1"] * 3,
+    "rbank": ["pR0", "pR1"],
+    "place": "_Ywi0:-2026 _Voneb0:-1950 _VTC0:-1946 _Gci0:-1943 _Vci1:-1939 _VCn0:-1936 _Vci2:-1910 _VDL0:-1878 _Gic0:-1852 _GiB0:-1824 _Ynbi0:-1809 _Gonef0:-1806 _VCn0.2:-1788 _Vcf0:-1784 _Vcf4:-1762 _Ynbi512:-1751 _Gi2560:-1726 _Gi160:-1694 _Vcf2:-1650 _VWb0:-1647 _VCk0:-1643 _Vzero0:-1639 _VBM0:-1614 _Vcf3:-1600 _VNB0:-1596 _SZV128:-1560 _Ynbi256:-1528 _VCk0.2:-1524 _VB240:-1242 _VSEL8:-1239 _VNB256:-1232 _Vcf1:-1174 _VSEL0:-1170 _VBM24:-1149 _VNB512:-1145 _Vcf6:-1055 _Stab2048:-1051 _VNB128:-1040 _SI320:-863 _GIf0:-827 _Ypooli0:-802 _SInb0:-795 _Ydi0:-773 _YMK0:-741 _SZV384:-730 _Stab4096:-683 _Ytab0:-603 _Gib0:-542 _Gia0:-484 _SIb0:-477 _SIh0:-434 _VD00:-365 _VRM0:-340 _SInf0:-329 _VNB384:-322 _Vtb0:-250 _Vta0:-235 _VCq0:-224 _VSEL16:-217 _Vpool512:-210 _GiJ0:-185 _Sic0:-159 _Vpool1024:-134 _VB20:-98 _VNB640:-80 _Vcf5:-62 _VBM8:-58 _VTC512:-33 _Gidd0:-11 _VKC0:7 _VKC16:32 _VSEL24:39 _YMK2048:83 _VKC24:115 _GONE0:129 _VZw0:187 _VBM16:202 _VKC8:310 _VB232:324 _Vlast0:328 _VTHR0:339 _VB28:346 _VB40:592 _VTC768:729 STU10:-842 STN0:-777 STU0:-755 raw0:-748 hk01:-733 hp01:-578 hn01:-495 ST1512:-448 u0:-445 hp12:-380 hn02:-354 VNU256:-343 STN256:-333 hk11:-325 ST1256:-315 hn00:-300 VNU0:-297 ht01:-293 VNU512:-282 hp00:-278 ht12:-260 STN512:-213 VOFF512:-199 VKX0:-195 ST10:-188 hn10:-181 hp02:-152 raw1:-138 VOFF256:-120 SSG0:-109 ht00:-105 VTU128:-76 VDY0:-73 VNU128:-65 VOFF0:-47 hn11:-44 u1:-37 k0:-22 hp10:-19 VNU384:-15 ht02:3 a01:14 hp11:18 VTN128:21 VTN384:25 VO116:28 ht11:36 SNB768:43 ht10:46 VNU640:68 SX0:72 hn12:75 dq0:79 VOFF384:86 SX1024:93 VTN640:97 SDY1024:101 PpR0:108 Ytab20:111 VDV2048:119 e1:126 VDV0:133 PpR0.2:140 VFK128:144 z10:151 VOFF128:155 VOFF640:162 VDV1024:166 dq1:169 VAV1024:180 VAV0:184 VUM8:209 e0:220 SAY0:231 SX2048:234 VE0:241 SAY3072:256 SAY1024:281 SDY2048:288 SAY3584:292 SAY1536:296 Gtab4096:299 SDI0:303 dc1:314 Yyp0:321 SX3072:332 VEE0:335 sDV0:342 sAY0:364 sAV0:368 sDV8:371 sDY8:375 SDY3072:379 VFK0:382 dc0:393 VDV3072:407 SXM384:411 VK0:415 PpR0.3:418 PpR0.4:425 VAV3072:429 VW10:433 VB224:436 fold2:444 sDV12:447 VW224:451 sAV12:454 k1:462 VB248:465 GNB512:469 VO10:480 sAY12:483 VW116:487 VNB768:490 VB256:494 VW2s24:498 VE128:501 sAV8:509 sAY8:512 VMK0:519 Sjunk0:527 VO224:530 VMS0:534 Yyx0:537 SCUT0:541 SXM0:545 VKX128:548 SZV0:559 z0:563 SSG128:570 Yyx2048:574 Ypool2512:577 VB216:581 Scf8:584 VW216:588 um0:599 VEE256:602 VK16:606 VUM0:610 VW28:613 VW20:617 VMK2048:624 VW2s0:628 SNB256:631 SRT0:638 SXM256:642 Yyc0:649 VO20:653 SDI128:664 SNB0:682 a02:689 VMS2048:693 Yyl0:696 Scf10:711 Yyq0:714 Vtab0:725 Vpool20:732 Vtab20:736 um1:743 SRT256:747 VW256:754 VW232:779 VW248:794 VW240:797 Yyz0:808 VW2s32:823 GNB640:833 VNB896:837 SZV256:844 count:859 z11:870 VW2s40:873 VO232:877 VO240:884 Vtab2048:888 VZV384:898 SCUT128:906 VpF10:909 VpF1128:913 VNB384:916 SNB128:931 STHR0:971 Vpool1024:992 Syp128:1000 YMK2048:1104 Syc128:1263 Vpool0:1277 YMK0:1285 Scf9:1389 Syz128:1595 Yyl512:1772 Syq128:2010",
+}
 
 F, H, I, U = "float32", "bfloat16", "int32", "uint16"
 SCRATCH = {
-    "tab": ("sbuf", [128, 4096], H), "X": ("sbuf", [128, 4096], H), "DV": ("sbuf", [128, 4096], H),
-    "DY": ("sbuf", [128, 4096], H), "AV": ("sbuf", [128, 16, 16, 16], H), "AY": ("sbuf", [128, 16, 16, 16], H),
+    "tab": ("sbuf", [128, 4112], H), "X": ("sbuf", [128, 4096], H), "DV": ("sbuf", [128, 4096], H),
+    "DY": ("sbuf", [128, 4096], H), "AV": ("sbuf", [128, 4096], H), "AY": ("sbuf", [128, 4096], H),
     "MK": ("sbuf", [128, 4096], H), "MS": ("sbuf", [128, 4096], H), "ONE": ("sbuf", [128, 2048], H),
     "pool": ("sbuf", [128, 2048], F), "pooli": ("sbuf", [128, 1024], I), "nbi": ("sbuf", [128, 768], I),
+    "tab2": ("sbuf", [128, 4096], H), "pool2": ("sbuf", [128, 2048], F),
     "ZV0": ("sbuf", [128, 512], H), "ZV1": ("sbuf", [128, 512], H),
-    "OFF": ("sbuf", [128, 768], U), "QI": ("sbuf", [128, 768], I), "QS": ("sbuf", [128, 768], I),
-    "N32": ("sbuf", [128, 768], F), "T1": ("sbuf", [128, 256], F), "T2": ("sbuf", [128, 256], H),
-    "SG": ("sbuf", [128, 256], F), "E": ("sbuf", [128, 256], F), "FK": ("sbuf", [128, 256], F),
-    "SR": ("sbuf", [128, 16], F), "C32": ("sbuf", [128, 8], F),
-    "tab2": ("sbuf", [128, 2048], H), "pool2": ("sbuf", [128, 1024], F),
-    "DM": ("sbuf", [128, 16], I), "ic": ("sbuf", [128, 128], F), "idd": ("sbuf", [128, 128], F),
-    "K": ("sbuf", [128, 16], I), "W1": ("sbuf", [128, 32], I), "O1": ("sbuf", [128, 32], U),
-    "UM": ("sbuf", [128, 16], I), "W2": ("sbuf", [128, 64], I), "W2s": ("sbuf", [128, 64], F),
-    "O2": ("sbuf", [128, 64], U), "B2": ("sbuf", [128, 64], F),
-    "M": ("sbuf", [128, 256], H), "XI": ("sbuf", [128, 256], H), "DI": ("sbuf", [128, 256], H),
-    "D4": ("sbuf", [128, 16, 16, 16], H), "Zn2": ("sbuf", [128, 144], H), "RL": ("sbuf", [128, 512], F),
-    "I8k": ("sbuf", [128, 128], H), "In4k": ("sbuf", [128, 128], H),
-    "CUT": ("sbuf", [128, 256], H), "RT": ("sbuf", [128, 512], F), "TC": ("sbuf", [128, 1280], H),
-    "wi": ("sbuf", [128, 4], I), "di": ("sbuf", [128, 4], I), "ci": ("sbuf", [128, 8], I), "cf": ("sbuf", [128, 16], F),
-    "THR": ("sbuf", [128, 8], F), "junk": ("sbuf", [128, 16], F),
+    "OFF": ("sbuf", [128, 768], U), "NU": ("sbuf", [128, 768], F), "TN": ("sbuf", [128, 768], H),
+    "QI": ("sbuf", [128, 768], I), "QS": ("sbuf", [128, 768], I), "Cj": ("sbuf", [128, 128], H),
+    "T1": ("sbuf", [128, 768], F), "TU": ("sbuf", [128, 256], H), "TU1": ("sbuf", [128, 256], F),
+    "SG": ("sbuf", [128, 512], F), "E": ("sbuf", [128, 512], F), "FK": ("sbuf", [128, 512], F),
+    "KX": ("sbuf", [128, 512], F), "K": ("sbuf", [128, 32], I), "W1": ("sbuf", [128, 32], I),
+    "O1": ("sbuf", [128, 32], U), "UM": ("sbuf", [128, 16], I), "W2": ("sbuf", [128, 64], I),
+    "W2s": ("sbuf", [128, 64], F), "O2": ("sbuf", [128, 64], U), "B2": ("sbuf", [128, 64], F),
+    "XM": ("sbuf", [128, 512], H), "DI": ("sbuf", [128, 256], H), "CUT": ("sbuf", [128, 256], H),
+    "RT": ("sbuf", [128, 512], F), "EE": ("sbuf", [128, 512], F), "TC": ("sbuf", [128, 1280], H),
+    "wi": ("sbuf", [128, 4], I), "di": ("sbuf", [128, 4], I), "ci": ("sbuf", [128, 8], I),
+    "cf": ("sbuf", [128, 16], F), "THR": ("sbuf", [128, 8], F), "junk": ("sbuf", [128, 16], F),
     "iJ": ("sbuf", [128, 144], F), "iB": ("sbuf", [128, 128], F), "ia": ("sbuf", [128, 256], F),
-    "ib": ("sbuf", [128, 256], F),
-    "i16": ("sbuf", [128, 16], F), "B4": ("sbuf", [128, 16], F), "ta": ("sbuf", [128, 256], H), "tb": ("sbuf", [128, 256], H),
-    "Wb": ("sbuf", [128, 128], H), "Zp": ("sbuf", [128, 144], H), "Zn": ("sbuf", [128, 144], H), "Zw": ("sbuf", [128, 144], H),
+    "ib": ("sbuf", [128, 256], F), "ic": ("sbuf", [128, 128], F), "idd": ("sbuf", [128, 128], F),
+    "i16": ("sbuf", [128, 8], F), "i256": ("sbuf", [128, 8], F), "B4": ("sbuf", [128, 8], F),
+    "ta": ("sbuf", [128, 256], H), "tb": ("sbuf", [128, 256], H), "last": ("sbuf", [128, 8], U),
+    "BM": ("sbuf", [128, 32], F), "KC": ("sbuf", [128, 32], F), "RM": ("sbuf", [128, 128], H),
+    "SEL": ("sbuf", [128, 32], H), "Wb": ("sbuf", [128, 128], H), "Zw": ("sbuf", [128, 144], H),
     "onef": ("sbuf", [128, 128], F), "If": ("sbuf", [128, 128], F), "Inf": ("sbuf", [128, 128], F),
-    "Ib": ("sbuf", [128, 128], H), "I2": ("sbuf", [128, 128], H), "Inb": ("sbuf", [128, 128], H),
-    "Ih": ("sbuf", [128, 128], H), "Cq": ("sbuf", [128, 128], H), "I32": ("sbuf", [128, 128], F),
-    "Dh": ("sbuf", [128, 128], H), "Dl": ("sbuf", [128, 128], H),
-    "Cn": ("sbuf", [128, 128], H), "oneb": ("sbuf", [128, 128], H), "zero": ("sbuf", [128, 128], H),
-    "D0": ("sbuf", [128, 136], F), "DL": ("sbuf", [128, 136], F),
+    "I32": ("sbuf", [128, 128], F), "Ib": ("sbuf", [128, 128], H), "Inb": ("sbuf", [128, 128], H),
+    "Ih": ("sbuf", [128, 128], H), "Cq": ("sbuf", [128, 128], H), "Cn": ("sbuf", [128, 128], H),
+    "Ck": ("sbuf", [128, 128], H), "oneb": ("sbuf", [128, 384], H), "zero": ("sbuf", [128, 128], H),
+    "D0": ("sbuf", [128, 128], F), "DL": ("sbuf", [128, 128], F),
 }
 for _t in range(VIS + 1):
     SCRATCH["NB%d" % _t] = ("sbuf", [128, 1024], F)
-for _n in ("pD0", "pD1", "pU", "pA", "pB", "pF", "pR0", "pR1"):
+for _n in ("pE0", "pE1", "pH0", "pH1", "pF0", "pF1", "pR0", "pR1"):
     SCRATCH[_n] = ("psum", [128, 512], F)
 DRAM = {"xt": H, "zt": H, "ch": I, "pa": I, "vi": I, "pl": I, "wt": I, "de": I,
         "yc": F, "yp": F, "yq": F, "yl": F, "yx": H, "yz": H}
@@ -71,14 +73,9 @@ def dtype(name):
     return DRAM[name] if name in DRAM else SCRATCH[name][2]
 
 
-def R(name, lo, hi, step=1, parts=None):
+def R(name, lo, hi, step=1, parts=(0, 128)):
     return {"ref": name, "lo": lo, "hi": hi, "n": len(range(lo, hi, step)),
-            "ix": (slice(None) if parts is None else slice(*parts), slice(lo, hi) if step == 1 else slice(lo, hi, step))}
-
-
-def R4(name, c0, c1, r=None):
-    ix = (slice(None), slice(c0, c1)) if r is None else (slice(None), slice(c0, c1), r)
-    return {"ref": name, "lo": 256 * c0, "hi": 256 * c1, "n": (c1 - c0) * (256 if r is None else 16), "ix": ix}
+            "ix": (slice(*parts), slice(lo, hi) if step == 1 else slice(lo, hi, step))}
 
 
 def IND(win, off):
@@ -90,16 +87,15 @@ def isref(a):
 
 
 def psum(a):
-    return a["ref"][0] == "p" and a["ref"] in SCRATCH and SCRATCH[a["ref"]][0] == "psum"
+    return a["ref"] in SCRATCH and SCRATCH[a["ref"]][0] == "psum"
 
 
-CY, PCY, LAT = 1.04, 0.55, 120.0
-
-
-def program():
+def program(P):
     ops, visit, seen = [], [-1], {}
+    chunks, pieces = P["chunks"], P["pieces"]
+    VIS = P.get("visits", 5)
 
-    def add(eng, kind, args, dur, **kw):
+    def add(eng, kind, args, cost, tag=None, **kw):
         rd, wr = [], []
         for call in (args if kind == "mm" else [args]):
             for j, a in enumerate(call):
@@ -109,26 +105,26 @@ def program():
                         rd.append(a["off"])
         if kw.get("accum") is not None:
             wr.append(kw["accum"])
-        op = {"eng": eng, "kind": kind, "args": args, "dur": dur, "rd": rd, "wr": wr}
+        op = {"eng": eng, "kind": kind, "args": args, "cost": cost, "rd": rd, "wr": wr, "acc": False}
         op.update(kw)
         name = wr[0]["ref"]
         name = name[:2] if name[:2] in ("NB", "ZV", "pR") else name
-        base = "%s%s%s%d" % ("" if visit[0] >= 0 else "s", eng, name, 0 if name == "THR" else wr[0]["lo"])
+        base = tag or "%s%s%d" % (eng, name, 0 if name == "THR" else wr[0]["lo"])
         seen[(visit[0], base)] = seen.get((visit[0], base), 0) + 1
-        op["tag"] = "%s.%d" % (base, seen[(visit[0], base)])
+        op["tag"] = base if seen[(visit[0], base)] == 1 else "%s.%d" % (base, seen[(visit[0], base)])
         op["visit"] = visit[0]
         ops.append(op)
         return op
 
     def cost(out, ins, two=False):
         if "off" in out:
-            return 50 + 3.8 * CY * out["n"]
+            return (50, 0, 0, out["n"], 0)
         if "off" in ins[0]:
-            return 55 + 1.56 * CY * ins[0]["n"]
+            return (50, 0, ins[0]["n"], 0, 0)
         f = 0.5 if all(SIZE[dtype(a["ref"])] == 2 for a in [out] + ins) else 1.0
         if two:
             f = 1.0 if any(psum(a) for a in ins) else 2.0
-        return 30 + CY * max(64, f * out["n"])
+        return (30, max(64, f * out["n"]), 0, 0, 0)
 
     def cp(out, a):
         add("V", "cp", [out, a], cost(out, [a]))
@@ -146,21 +142,26 @@ def program():
         add("V", "ms", [out, v], cost(out, [out]))
 
     def act(out, a, fn, bias=0.0, scale=1.0, accum=None):
-        d = 65 + 1.56 * CY * a["n"] if "off" in a else 40 + CY * max(64, a["n"])
-        add("S", "act", [out, a, fn, bias, scale], d, accum=accum)
+        c = (65, 0, a["n"], 0, 0) if "off" in a else (40, max(64, a["n"]), 0, 0, 0)
+        add("S", "act", [out, a, fn, bias, scale], c, accum=accum)
 
-    def mm(calls, **kw):
-        d = 40 + sum(max(64, c[0]["n"]) * (4 if dtype(c[1]["ref"]) == F else 1) * PCY for c in calls)
-        add("P", "mm", calls, d, **kw)
+    def mm(calls, tag=None, acc=False, opens=False):
+        cyc = sum(max(min(64, c[1]["n"]), c[0]["n"]) * (4 if dtype(c[1]["ref"]) == F else 1) for c in calls)
+        op = add("P", "mm", [list(c) for c in calls], (40, 0, 0, 0, cyc), tag=tag, acc=acc)
+        if opens:
+            op["wr"].append(R(calls[0][0]["ref"], 0, 512))
 
-    def group(out, pairs, start=True, stop=True):
-        return [[out, a, b, start and j == 0, stop and j == len(pairs) - 1] for j, (a, b) in enumerate(pairs)]
+    def group(out, pairs, start=True):
+        return [(out, a, b, start and j == 0) for j, (a, b) in enumerate(pairs)]
 
     def iota(out, pattern, base, cm):
-        add("G", "iota", [out, pattern, base, cm], 140 + 2 * CY * out["n"])
+        add("G", "iota", [out, pattern, base, cm], (130, 2 * out["n"], 0, 0, 0))
+
+    def gcopy(out, a, diagonal=False):
+        add("G", "sel", [out, a, diagonal], (170, 2 * out["n"], 0, 0, 0))
 
     def dma(q, out, a):
-        add(q, "dma", [out, a], 60, bytes=128 * out["n"] * SIZE[dtype(out["ref"])])
+        add(q, "dma", [out, a], (60, 0, 0, 0, 0), bytes=128 * out["n"] * SIZE[dtype(out["ref"])])
 
     def gather(eng, out, src):
         if eng == "V":
@@ -168,10 +169,20 @@ def program():
         else:
             act(out, src, ACT.Copy)
 
+    def rounded(eng, out, src, unit, tmp):
+        if eng == "V":
+            ts(out, src, unit * MAGIC, ALU.add, unit * MAGIC, ALU.subtract)
+        else:
+            act(tmp, src, ACT.Identity, MAGIC, 1.0 / unit)
+            act(out, tmp, ACT.Identity, -unit * MAGIC, float(unit))
+
     col = lambda j: R("cf", j, j + 1)
-    G16, KF, C16, C4, CN, WF = (col(j) for j in range(6))
+    G16, KF, C16, C4, WF, K0, K1, CNT = (col(j) for j in range(8))
+    CN = col(11)
     M128 = lambda name: R(name, 0, 128)
-    lanes = [(16 * a, 16 * b) for a, b in CHUNKS]
+    low = lambda name, n: R(name, 0, n, parts=(0, 64))
+    lanes = [(16 * a, 16 * b) for a, b in chunks]
+    SELECT = {1: R("SEL", 0, 8), -1: R("SEL", 8, 16), 2: R("SEL", 16, 24), -2: R("SEL", 24, 32)}
 
     def zv(t, x, part):
         l0, l1 = lanes[x]
@@ -183,22 +194,30 @@ def program():
 
     dma("Y", R("wi", 0, 1), R("wt", 0, 1))
     for x, (l0, l1) in enumerate(lanes):
-        dma("S", zv(0, x, 0), R("zt", l0, l1))
+        dma("S", zv(0, x, 1), R("zt", l0, l1))
     dma("Y", R("nbi", 256, 512), R("ch", 0, 256))
     dma("Y", R("tab", 0, 2048), R("xt", 0, 2048))
     dma("S", R("tab", 2048, 4096), R("xt", 2048, 4096))
+    margin = 16 if set("SV") & set(P["t"]) else 0
+    if margin:
+        dma("S", R("tab", 4096, 4112), R("xt", 0, 16))
     dma("Y", R("nbi", 512, 768), R("vi", 0, 256))
     dma("Y", R("nbi", 0, 256), R("pa", 0, 256))
     dma("Y", R("di", 0, 1), R("de", 0, 1))
     dma("Y", R("pooli", 0, 1024), R("pl", 0, 1024))
     iota(R("ci", 0, 1), [[0, 1]], 0, 1)
     iota(M128("iB"), [[16, 8], [0, 16]], 0, 0)
+    iota(M128("ic"), [[0, 8], [1, 16]], 0, 0)
+    for name, base, users in (("Ck", -6144.0, "SV"), ("Cj", -8192.0, "I")):
+        if set(users) & set(P["t"]):
+            ts(R(name, 0, 128, parts=(0, 32)), R("ic", 0, 128, parts=(0, 32)), 32.0, ALU.mult, base, ALU.add)
+            ts(R(name, 0, 128, parts=(32, 64)), R("ic", 0, 128, parts=(32, 64)), 5.0, ALU.mult)
     iota(M128("onef"), [[0, 128]], 1, 0)
-    add("G", "sel", [M128("If"), M128("onef")], 170 + 2 * CY * 128)
+    gcopy(M128("If"), M128("onef"), True)
+    iota(R("i16", 0, 8), [[16, 8]], 0, 0)
+    iota(R("i256", 0, 8), [[256, 8]], 0, 0)
     iota(R("iJ", 0, 144), [[1, 144]], -15, 0)
-    iota(M128("ic"), [[-3840, 8], [1, 16]], 28672, 0)
     iota(M128("idd"), [[32, 8], [0, 16]], 1, 0)
-    iota(R("i16", 0, 8), [[256, 8]], 0, 0)
     iota(R("ia", 0, 256), [[0, 16], [1, 16]], 0, 0)
     iota(R("ib", 0, 256), [[-1, 16], [0, 16]], 15, 0)
     iota(R("ONE", 0, 2048), [[0, 2048]], 1, 0)
@@ -208,48 +227,41 @@ def program():
     cp(KF, R("ci", 2, 3))
     ts(C16, R("ci", 2, 3), 16.0, ALU.mult)
     ts(C4, R("ci", 2, 3), 4.0, ALU.mult)
-    ts(CN, R("ci", 2, 3), 1184.0, ALU.mult, -262144.0, ALU.add)
+    ts(K0, R("ci", 1, 2), -65536.0, ALU.mult)
+    ts(K1, R("ci", 1, 2), 4096.0, ALU.mult, 2048.0 * 18 + 15 + 15 / 32, ALU.add)
+    if "J" in P["t"]:
+        ts(CN, R("ci", 2, 3), 1184.0, ALU.mult, -262144.0, ALU.add)
     cp(WF, R("wi", 0, 1))
-    ts(R("THR", 0, 1), R("di", 0, 1), 1.0 - 1.0 / 65536, ALU.add)
-    if RS:
-        iota(R("C32", 0, 8), [[-32, 8]], 0, 0)
+    ts(R("THR", 0, 1), R("di", 0, 1), 1.0, ALU.add, 32768.0, ALU.mult)
     ts(M128("Wb"), M128("iB"), G16, ALU.is_equal, WF, ALU.mult)
     ms(R("Cn", 0, 128, parts=(0, 32)), -64.0)
     ms(R("Cn", 0, 128, parts=(32, 64)), 1.0 / 64)
-    ms(M128("oneb"), 1.0)
-    act(M128("Ib"), M128("If"), ACT.Copy)
-    act(M128("Inf"), M128("If"), ACT.Copy, scale=-1.0)
-    act(M128("Inb"), M128("If"), ACT.Copy, scale=-1.0)
-    if len(ZV) < 2:
-        act(M128("I2"), M128("If"), ACT.Copy, scale=2.0)
-    if any(SEL):
-        act(M128("I8k"), M128("If"), ACT.Copy, scale=8192.0)
-        act(M128("In4k"), M128("If"), ACT.Copy, scale=-4096.0)
-    if Y2:
-        ts(R("Zn2", 0, 144), R("iJ", 0, 144), G16, ALU.is_equal, -2.0, ALU.mult)
-    if ZV:
-        act(M128("Ih"), M128("If"), ACT.Copy, scale=0.5)
-        ms(R("Cq", 0, 128, parts=(0, 64)), -1.0 / 256)
-    if NP:
-        ts(col(6), R("ci", 2, 3), 1024.0, ALU.mult, -262144.0, ALU.add)
-        ts(col(7), R("ci", 2, 3), 160.0, ALU.mult)
-        act(M128("I32"), M128("If"), ACT.Copy, scale=32.0)
-        act(M128("Dh"), M128("If"), ACT.Copy, scale=col(6))
-        act(M128("Dl"), M128("If"), ACT.Copy, scale=col(7))
-    ts(R("Zp", 0, 144), R("iJ", 0, 144), G16, ALU.is_equal)
-    ts(R("Zn", 0, 144), R("iJ", 0, 144), G16, ALU.is_equal, -1.0, ALU.mult)
+    ms(R("oneb", 0, 384), 1.0)
+    ms(low("Cq", 128), -1.0 / 256)
+    ms(M128("zero"), 0.0)
+    for name, s in (("Inb", -1.0), ("I32", 32.0), ("Ib", 1.0), ("Inf", -1.0), ("Ih", 0.5)):
+        if name != "I32" or set("SVI") & set(P["t"]):
+            act(M128(name), M128("If"), ACT.Copy, scale=s)
+    for s, a in SELECT.items():
+        ts(a, R("i16", 0, 8), G16, ALU.is_equal, float(s), ALU.mult)
     ts(R("Zw", 0, 144), R("iJ", 0, 144), G16, ALU.is_equal, WF, ALU.mult)
+    ts(M128("RM"), M128("ic"), KF, ALU.is_equal)
     act(M128("ic"), M128("ic"), ACT.Copy, scale=1.0 / 32768)
     tt(M128("D0"), M128("ic"), M128("idd"), ALU.add)
     ms(M128("DL"), 16.0 / 32768)
-    ts(col(9), R("ci", 2, 3), 16.0, ALU.mult, 1807.0, ALU.add)
-    ms(M128("zero"), 0.0)
-    ts(R("B4", 0, 8), R("i16", 0, 8), 0.25, ALU.mult, C4, ALU.add)
-    for c0, c1 in CHUNKS:
+    ts(R("last", 0, 8), R("i16", 0, 8), 15.0, ALU.add)
+    ts(R("B4", 0, 8), R("i256", 0, 8), 0.25, ALU.mult, C4, ALU.add)
+    for x, (c0, c1) in enumerate(chunks):
         C = c1 - c0
-        ts(R("B2", 4 * c0, 4 * c0 + C), R("i16", 0, C), C16, ALU.add)
+        ts(R("BM", 2 * c0, 2 * c0 + C), R("i16", 0, C), G16, ALU.is_equal, 32768.0, ALU.mult)
+        ts(R("BM", 2 * c0 + C, 2 * c1), R("i16", 0, C), G16, ALU.is_equal, -2048.0, ALU.mult)
+        ts(R("KC", 2 * c0, 2 * c0 + C), R("i256", 0, C), K0, ALU.add)
+        ts(R("KC", 2 * c0 + C, 2 * c1), R("i256", 0, C), K1, ALU.add)
+        ts(R("B2", 4 * c0, 4 * c0 + C), R("i256", 0, C), C16, ALU.add)
         ms(R("B2", 4 * c0 + C, 4 * c0 + 2 * C), 0.0)
         dma("Y", R("MK", 256 * c0, 256 * c1), R("ONE", 0, 256 * C))
+        if C < 8:
+            ms(R("FK", 128 * x, 128 * x + 128), 0.0)
     ms(R("TC", 0, 512), 0.0)
     ms(R("TC", 768, 1280), 0.0)
     ts(R("ta", 0, 256), R("ia", 0, 256), KF, ALU.is_le)
@@ -261,185 +273,227 @@ def program():
     for j in range(2):
         cp(R("pool", 512 * j + 512, 512 * j + 1024), R("pooli", 512 * j, 512 * j + 512))
 
-    TAB = R("tab", 0, 4096)
-    sel = lambda name, r: R(name, 15 - r, 143 - r)
-    nr3 = [0]
+    TAB = R("tab", 0, 4096 + margin)
+    nr = [0]
     for t in range(VIS):
         last = t == VIS - 1
         visit[0] = t
         if last:
-            dma("Y", R("tab2", 0, 2048), R("tab", 0, 2048))
-            dma("Y", R("pool2", 512, 1024), R("pool", 512, 1024))
+            c = chunks[-1][0]
+            dma("Y", R("tab2", 0, 256 * c), R("tab", 0, 256 * c))
+            dma("Y", R("pool2", 512, 512 + 64 * c), R("pool", 512, 512 + 64 * c))
         for x, (l0, l1) in enumerate(lanes):
             n = l1 - l0
-            bank = ("pA", "pB")[x % 2]
-            z = zv(t, x, 0)
-            mm(group(R("pU", 0, n), [(M128("Wb"), z), (R("Cn", 0, 128, parts=(0, 64)), R("oneb", 0, n, parts=(0, 64)))]))
-            if x in UV:
-                ts(R("T2", l0, l1), R("pU", 0, n), 4096 * MAGIC, ALU.add, 4096 * MAGIC, ALU.subtract)
-                mm(group(R(bank, 0, n), [(M128("Wb"), z), (M128("Inb"), R("T2", l0, l1))]))
-            else:
-                act(R("T1", l0, l1), R("pU", 0, n), ACT.Identity, MAGIC, 1.0 / 4096)
-                act(R("T2", l0, l1), R("T1", l0, l1), ACT.Identity, 4096 * MAGIC, -4096.0)
-                mm(group(R(bank, 0, n), [(M128("Wb"), z), (M128("Ib"), R("T2", l0, l1))]))
+            pE = "pE%d" % (x % 2)
+            z, raw, u, tu = zv(t, x, 1), R(pE, 256, 256 + n), R(pE, 384, 384 + n), R("TU", l0, l1)
+            mm(group(raw, [(low("Cn", 128), low("oneb", n)), (M128("Wb"), z)]), tag="raw%d" % x)
+            rounded(P["u"][x], tu, raw, 4096, R("TU1", l0, l1))
+            mm(group(u, [(M128("Wb"), z), (M128("Inb"), tu)]), tag="u%d" % x)
             for s in (1, 2, 0):
                 a, b = 256 * s + l0, 256 * s + l1
-                P, N = R(bank, 128 * (s + 1), 128 * (s + 1) + n), R("N32", a, b)
-                if 3 * x + s in NP:
-                    P, N = N, P
-                    mm(group(N, [(M128("I32"), nb(t, s, x)), (M128("Dh"), R("oneb", 0, n)), (M128("Dl"), R("oneb", 0, n))]))
+                Q, how = R(P["hbank"][3 * x + s], s * n, s * n + n), P["t"][3 * x + s]
+                tt(R("NU", a, b), nb(t, s, x), u, ALU.mult)
+                if how in "IJ":
+                    if how == "I":
+                        mm(group(Q, [(low("Cj", 128), low("oneb", n)), (M128("I32"), nb(t, s, x))]), tag="hn%d%d" % (x, s))
+                    else:
+                        act(R("T1", a, b), nb(t, s, x), ACT.Identity, CN, 32.0)
+                        ops[-2]["args"][0] = ops[-2]["wr"][0] = Q
+                    tt(R("QI", a, b), R("NU" if how == "I" else "T1", a, b), Q, ALU.add)
+                    ts(R("QS", a, b), R("QI", a, b), 5, ALU.arith_shift_right, 4095, ALU.bitwise_and)
+                    cp(R("OFF", a, b), R("QS", a, b))
                 else:
-                    act(N, nb(t, s, x), ACT.Identity, CN, 32.0)
-                tt(P, nb(t, s, x), R(bank, 0, n), ALU.mult)
-                tt(R("QI", a, b), P, N, ALU.add)
-                ts(R("QS", a, b), R("QI", a, b), 5, ALU.arith_shift_right, 4095, ALU.bitwise_and)
-                cp(R("OFF", a, b), R("QS", a, b))
-        for pc, (a, b) in enumerate(zip(CUTS[:-1], CUTS[1:])):
-            if True:
-                big = lambda name, u=a, v=b: R(name, 256 * u, 256 * v)
-                off = lambda s: R("OFF", 256 * s + 16 * a, 256 * s + 16 * b)
-                bank = ("pD0", "pD1")[pc % 2]
-                whole = R(bank, 0, 512)
-                D = R(bank, 0, 16 * (b - a))
-                gather("V" if pc in (XV if t else XV0) else "S", big("X"), IND(TAB, off(1)))
-                sums = []
-                for s, dn, an, zn, by_s in ((2, "DV", "AV", "Zp", a // 8 in V3), (0, "DY", "AY", "Zn", pc in R3)):
-                    pairs = [(sel(zn, r), R4(an, a, b, r)) for r in range(16)]
-                    if by_s:
-                        gather("S", big(dn), IND(TAB, off(s)))
+                    terms = [(low("Ck", 128), low("oneb", n)), (M128("I32"), nb(t, s, x)), (M128("If"), R("NU", a, b))]
+                    mm(group(Q, terms), tag="hp%d%d" % (x, s))
+                    rounded(how, R("TN", a, b), Q, 131072, R("T1", a, b))
+                    mm(group(Q, terms + [(M128("Inb"), R("TN", a, b))]), tag="ht%d%d" % (x, s))
+                    ts(R("OFF", a, b), Q, 1.0 / 32, ALU.mult, 2048 - 31 / 64, ALU.add)
+        for x, (c0, c1) in enumerate(chunks):
+            n = 16 * (c1 - c0)
+            pE = "pE%d" % (x % 2)
+            mine = [pc for pc, (a, b) in enumerate(pieces) if c0 <= a < c1]
+            mm(group(R(pE, 0, 128), [(low("zero", 128), low("oneb", 128))]), tag="e%d" % x, opens=True)
+
+            def sums(name, a, b, w):
+                at = (16 * (a - c0), 16 * (b - c0))
+                for j in range(P["split"]):
+                    mm([(R(pE, k, 128, 16, parts=at), R(name, 256 * a + k, 256 * b, 16), SELECT[w], False)
+                        for k in range(j, 16, P["split"])], tag="s%s%d" % (name, a), acc=True)
+
+            for pc in mine:
+                a, b = pieces[pc]
+                gather(P["x" if t else "x0"][pc], R("X", 256 * a, 256 * b), IND(TAB, R("OFF", 256 + 16 * a, 256 + 16 * b)))
+            for s, key, dn, an, w in ((2, "v", "DV", "AV", 1), (0, "y", "DY", "AY", -1)):
+                for pc in mine:
+                    a, b = pieces[pc]
+                    big = lambda name, u=a, v=b: R(name, 256 * u, 256 * v)
+                    src, route = IND(TAB, R("OFF", 256 * s + 16 * a, 256 * s + 16 * b)), P[key][pc]
+                    if route in "VM":
+                        tt(big(dn), src, big("X"), ALU.subtract)
+                        if route == "V":
+                            ts(big(an), big(dn), 0.0, ALU.max, 2.0, ALU.mult)
+                        else:
+                            act(big(an), big(dn), ACT.Abs)
+                    elif route == "S":
+                        gather("S", big(dn), src)
                         for u in range(a, b, 2):
                             v = min(u + 2, b)
-                            pr = R(("pR0", "pR1")[nr3[0] % 2], 0, 256 * (v - u))
-                            nr3[0] += 1
-                            mm(group(pr, [(M128("Ib"), big(dn, u, v)), (M128("Inb"), big("X", u, v))]))
-                            act(R4(an, u, v), pr, ACT.Abs)
-                    elif s == 0 and pc in Y2:
-                        tt(R4("D4", a, b), IND(TAB, off(s)), big("X"), ALU.subtract)
-                        ts(R4(an, a, b), R4("D4", a, b), 0.0, ALU.max)
-                        pairs = ([(sel("Zp", r), R4("D4", a, b, r)) for r in range(16)]
-                                 + [(sel("Zn2", r), R4(an, a, b, r)) for r in range(16)])
+                            pr = R(P["rbank"][nr[0] % len(P["rbank"])], 0, 256 * (v - u))
+                            nr[0] += 1
+                            mm(group(pr, [(M128("Inb"), big("X", u, v)), (M128("Ib"), big(dn, u, v))]))
+                            act(big(an, u, v), pr, ACT.Abs)
                     else:
-                        tt(big(dn), IND(TAB, off(s)), big("X"), ALU.subtract)
-                        act(R4(an, a, b), big(dn), ACT.Abs)
-                    sums.append(pairs)
-                if pc in YF:
-                    sums.reverse()
-                for j, pairs in enumerate(sums):
-                    mm(group(D, pairs, j == 0, j == 1))
-                    ops[-1]["wr"].append(whole)
-                act(R("SG", 16 * a, 16 * b), D, ACT.Sign, scale=-1.0)
-        for x, (c0, c1) in enumerate(CHUNKS):
+                        gather("S" if route == "F" else "V", big(dn), src)
+                        both = P["pair"] and P["v"][pc] in "FG" and P["y"][pc] in "FG"
+                        if not both:
+                            add("G", "fold", [big(an), big("X"), big(dn)], (1000, 0, 0, 0, 0), tag="fold%s%d" % (key, pc),
+                                bytes=128 * 512 * (b - a))
+            for pc in mine:
+                if P["pair"] and P["v"][pc] in "FG" and P["y"][pc] in "FG":
+                    a, b = pieces[pc]
+                    big = lambda name: R(name, 256 * a, 256 * b)
+                    op = add("G", "fold", [big("AV"), big("X"), big("DV"), big("AY"), big("X"), big("DY")], (1000, 0, 0, 0, 0),
+                             tag="fold%d" % pc, bytes=128 * 1024 * (b - a))
+                    op["wr"].append(op["rd"].pop(2))
+            for s, key, dn, an, w in ((2, "v", "DV", "AV", 1), (0, "y", "DY", "AY", -1)):
+                runs = []
+                for pc in mine:
+                    kind = {"V": "V", "M": "A", "S": "A", "F": "F", "G": "F"}[P[key][pc]]
+                    if runs and runs[-1][0] == kind and P["whole"][x] == "1":
+                        runs[-1][2] = pieces[pc][1]
+                    else:
+                        runs.append([kind, pieces[pc][0], pieces[pc][1]])
+                for kind, a, b in runs:
+                    if kind != "A":
+                        sums(dn, a, b, -w)
+                    if kind == "F":
+                        sums(an, a, b, 2 * w)
+                if all(r[0] != "F" for r in runs) and P["whole"][x] == "1":
+                    sums(an, c0, c1, w)
+                else:
+                    for kind, a, b in runs:
+                        if kind != "F":
+                            sums(an, a, b, w)
+            for pc in mine:
+                fv, fy = P["v"][pc] in "FG", P["y"][pc] in "FG"
+                if fv != fy:
+                    sums("X", pieces[pc][0], pieces[pc][1], -1 if fv else 1)
+            adds = [op for op in ops if op["acc"] and op["visit"] == t and op["wr"][0]["ref"] == pE]
+            wide = [op for op in adds if op["wr"][0]["ix"][0] == slice(0, n)]
+            if wide and len(wide) < len(adds):
+                for op in wide[-P["split"]:]:
+                    ops.remove(op)
+                    ops.append(op)
+                    op["acc"] = False
+            act(R("SG", 128 * x, 128 * x + 128, parts=(0, n)), R(pE, 0, 128, parts=(0, n)), ACT.Sign, scale=-1.0)
+        for x, (c0, c1) in enumerate(chunks):
             C = c1 - c0
             l0, l1 = lanes[x]
             n = l1 - l0
+            pE, pF = "pE%d" % (x % 2), "pF%d" % (x % 2)
             ln = lambda name: R(name, l0, l1)
+            el = lambda name: R(name, 128 * x, 128 * x + 128, parts=(0, n))
             sm = lambda name, w=1, p0=0, p1=None: R(name, w * c0 + p0 * C, w * c0 + (w if p1 is None else p1) * C)
             big = lambda name: R(name, 256 * c0, 256 * c1)
-            K = sm("K")
-            oi, oj = sm("O1", 2, 0, 1), sm("O1", 2, 1, 2)
-            scan(ln("E"), R("D0", 0, n), ln("SG"), ALU.max, ALU.add)
-            scan(ln("FK"), R("DL", 0, n), ln("E"), ALU.add, ALU.max)
-            ts(K, R("FK", l0 + 15, l1, 16), 32768.0, ALU.mult)
-            ts(sm("W1", 2, 0, 1), K, 0x70F, ALU.bitwise_and)
-            ts(oi, sm("W1", 2, 0, 1), C16, ALU.add)
-            ts(sm("W1", 2, 1, 2), K, 4, ALU.logical_shift_right, 0x70F, ALU.bitwise_and)
-            ts(oj, sm("W1", 2, 1, 2), -1.0, ALU.mult, col(9), ALU.add)
-            if x not in RS:
-                ts(sm("DM"), K, 15, ALU.logical_shift_right, 31, ALU.bitwise_and)
+            first = c0 < 8
+            oi, xi, m = sm("O1", 2, 0, 1), R("XM", 2 * l0, 2 * l0 + n), R("XM", 2 * l0 + n, 2 * l1)
+            scan(el("E"), R("D0", 0, 128, parts=(0, n)), el("SG"), ALU.max, ALU.add)
+            scan(el("FK"), R("DL", 0, 128, parts=(0, n)), el("E"), ALU.add, ALU.max)
+            tt(R("KX", 128 * x, 128 * x + 128), IND(R("FK", 128 * x, 128 * x + 128), R("last", 0, 8)), M128("RM"), ALU.mult)
+            pk = R(pE, 128, 128 + 2 * C)
+            mm(group(pk, [(el("KX"), R("BM", 2 * c0, 2 * c1, parts=(0, n)))]), tag="k%d" % x)
+            tt(sm("K", 2), pk, sm("KC", 2), ALU.add)
+            ts(sm("W1", 2), sm("K", 2), 0x70F, ALU.bitwise_and)
+            ts(sm("O1", 2), sm("W1", 2), C16, ALU.add)
             cp(IND(big("MK"), oi), R("zero", 0, n))
             scan(big("MS"), big("MK"), big("X"), ALU.mult, ALU.max)
             if not last:
                 dma("Y", big("MK"), R("ONE", 0, 256 * C))
-            ts(sm("W2", 4, 3, 4), K, 255, ALU.bitwise_and)
-            if x in RS:
-                g1, g2 = R("pU", 160 + c0, 160 + c1), R("pU", 176 + c0, 176 + c1)
-                mm(group(g1, [(M128("If"), R("FK", l0 + 15, l1, 16)), (M128("If"), R("C32", 0, C))]))
-                act(sm("SR"), g1, ACT.Sign, R("THR", t, t + 1), -1.0)
-                act(sm("B2", 4, 3, 4), sm("SR"), ACT.Identity, 256.0, (-256.0, 256.0)[x])
-                mm(group(g2, [(M128("If"), sm("B2", 4, 3, 4)), (M128("If"), R("B4", 0, C))]))
-                act(sm("B2", 4, 2, 3), g2, ACT.Copy)
-            else:
-                ts(sm("B2", 4, 3, 4), sm("DM"), R("THR", t, t + 1), (ALU.is_ge, ALU.is_lt)[x], 512.0, ALU.mult)
-                tt(sm("B2", 4, 2, 3), sm("B2", 4, 3, 4), R("B4", 0, C), ALU.add)
-            gather("S", ln("XI"), IND(big("X"), oi))
+            ts(sm("W2", 4, 3, 4), sm("K", 2, 0, 1), 255, ALU.bitwise_and)
+            ts(sm("B2", 4, 3, 4), sm("K", 2, 0, 1), R("THR", t, t + 1), ALU.is_ge if first else ALU.is_lt, 512.0, ALU.mult)
+            tt(sm("B2", 4, 2, 3), sm("B2", 4, 3, 4), R("B4", 0, C), ALU.add)
             gather("S", ln("DI"), IND(big("DV"), oi))
-            gather("V" if x in MV else "S", ln("M"), IND(big("MS"), oj))
-            um = R("pU", 128 + c0, 128 + c1)
-            mm(group(um, [(sel("Zw", r), R("M", l0 + r, l1, 16)) for r in range(16)]))
-            znew = R("ZV%d" % ((t + 1) % 2), 2 * l0, 2 * l1)
-            if x in ZV:
-                q4 = (R("Cq", 0, 128, parts=(0, 64)), R("oneb", 0, n, parts=(0, 64)))
-                mm(group(R("pF", 256 + n, 256 + 2 * n), [q4, (M128("Ih" if x in V3 else "Ib"), ln("XI")), (M128("Ih"), ln("DI"))])
-                   + group(R("pF", 256, 256 + n), [q4, (M128("Ih"), zv(t, x, 0)), (M128("Ih"), ln("M"))]))
-                ts(znew, R("pF", 256, 256 + 2 * n), MAGIC, ALU.add, MAGIC, ALU.subtract)
+            if P["apart"][x] == "1":
+                gather("S", xi, IND(big("X"), oi))
+                gather(P["m"][x], m, IND(big("MS"), sm("O1", 2, 1, 2)))
             else:
-                mm(group(R("pF", 256 + n, 256 + 2 * n), [(M128("Ib" if x in V3 else "I2"), ln("XI")), (M128("Ib"), ln("DI"))])
-                   + group(R("pF", 256, 256 + n), [(M128("Ib"), zv(t, x, 0)), (M128("Ib"), ln("M"))]))
-                rt = R("RT", 2 * l0, 2 * l1)
-                act(rt, R("pF", 256, 256 + 2 * n), ACT.Identity, MAGIC, 0.4999)
-                act(znew, rt, ACT.Identity, -MAGIC)
+                gather(P["m"][x], R("XM", 2 * l0, 2 * l1), IND(big("MS"), sm("O1", 2)))
+            um = R(pE, 160, 160 + C)
+            mm(group(um, [(R("Zw", 15 - r, 143 - r), R("XM", m["lo"] + r, m["hi"], 16)) for r in range(16)]), tag="um%d" % x)
+            quarter = (low("Cq", 128), low("oneb", n))
+            calls = group(R(pF, 256, 256 + n), [quarter, (M128("Ih"), ln("DI"))])
+            for pc, (a, b) in enumerate(pieces):
+                if c0 <= a < c1:
+                    u, v = 16 * (a - c0), 16 * (b - c0)
+                    calls += group(R(pF, 256 + u, 256 + v), [(M128("Ib" if P["v"][pc] in "VM" else "Ih"), R("XM", 2 * l0 + u, 2 * l0 + v))], False)
+            marks = group(R(pF, 256 + n, 256 + 2 * n), [quarter, (M128("Ih"), zv(t, x, 1)), (M128("Ih"), m)])
+            if P["apart"][x] == "1":
+                for j, part in enumerate((calls, marks)):
+                    mm(part, tag="z%d%d" % (x, j))
+                    rounded(P["z"][2 * x + j], zv(t + 1, x, j), R(pF, 256 + j * n, 256 + j * n + n), 1, R("RT", 2 * l0 + j * n, 2 * l0 + j * n + n))
+            else:
+                mm(calls + marks, tag="z%d" % x)
+                rounded(P["z"][2 * x], R("ZV%d" % ((t + 1) % 2), 2 * l0, 2 * l1), R(pF, 256, 256 + 2 * n), 1, R("RT", 2 * l0, 2 * l1))
             cp(sm("UM"), um)
             for j, bits in enumerate((15, 1023, 3)):
                 ts(sm("W2", 4, j, j + 1), sm("UM"), bits, ALU.bitwise_and)
-            for p0, p1 in (((3, 4), (0, 3)) if x in EC or last and x == 1 else ((0, 4),)):
+            cuts = [0] + [1] * (P["early"][x] == "1") + [3] * (P["cut"][x] == "1") + [4]
+            for p0, p1 in zip(cuts[:-1], cuts[1:]):
                 tt(sm("W2s", 4, p0, p1), sm("W2", 4, p0, p1), sm("B2", 4, p0, p1), ALU.add)
                 cp(sm("O2", 4, p0, p1), sm("W2s", 4, p0, p1))
+            gather("S", ln("CUT"), IND(R("TC", 0, 768) if first else R("TC", 512, 1280), sm("O2", 4, 3, 4)))
             gather("S", nb(t + 1, 0, x), IND(R("pool", 512, 1536), sm("O2", 4, 1, 2)))
-            gather("S", ln("CUT"), IND(R("TC", 512 * x, 512 * x + 768), sm("O2", 4, 3, 4)))
-            d1, d2 = R("pU", 256, 256 + n), R("pU", 384, 384 + n)
-            e1, e2 = R("pF", 0, n), R("pF", 128, 128 + n)
-            up = [(M128("I8k"), ln("CUT"))] if SEL[x] else []
-            mm(group(d1, [(M128("If"), nb(t, 0, x)), (M128("Inf"), nb(t, 1, x))] + up)
-               + group(d2, [(M128("If"), nb(t, 1, x)), (M128("Inf"), nb(t, 2, x))] + up))
-            if SEL[x] == 0:
-                tt(e2, d2, ln("CUT"), ALU.mult)
-                tt(e1, d1, ln("CUT"), ALU.mult)
-                tt(nb(t + 1, 3, x), e2, nb(t, 2, x), ALU.add)
-                tt(nb(t + 1, 1, x), e1, nb(t, 1, x), ALU.add)
-            else:
-                r1, r2 = R("RL", 2 * l0, 2 * l0 + n), R("RL", 2 * l0 + n, 2 * l1)
-                act(R("RL", 2 * l0, 2 * l1), R("pU", 256, 512), ACT.Relu, -4096.0)
-                down = (M128("In4k"), ln("CUT"))
-                if SEL[x] == 1:
-                    mm(group(e1, [(M128("If"), nb(t, 1, x)), down]) + group(e2, [(M128("If"), nb(t, 2, x)), down]))
-                    tt(nb(t + 1, 3, x), e2, r2, ALU.add)
-                    tt(nb(t + 1, 1, x), e1, r1, ALU.add)
+            d1, d2 = R(pF, 0, n), R(pF, 128, 128 + n)
+            mm(group(d1, [(M128("If"), nb(t, 0, x)), (M128("Inf"), nb(t, 1, x))]), tag="dc%d" % x)
+            mm(group(d2, [(M128("If"), nb(t, 1, x)), (M128("Inf"), nb(t, 2, x))]), tag="dq%d" % x)
+            for d, old, new in ((d2, 2, 3), (d1, 1, 1)):
+                if old == 2 and not last:
+                    tt(nb(t + 1, 3, x), d, ln("CUT"), ALU.mult)
+                    add("G", "send", [nb(t + 1, 2, x), nb(t + 1, 3, x), nb(t, 2, x)], (1000, 0, 0, 0, 0), bytes=128 * n * 8)
+                elif P["add"][x] == "V":
+                    tt(d, d, ln("CUT"), ALU.mult)
+                    tt(nb(t + 1, new, x), d, nb(t, old, x), ALU.add)
                 else:
-                    mm(group(e1, [(M128("If"), nb(t, 1, x)), down, (M128("If"), r1)])
-                       + group(e2, [(M128("If"), nb(t, 2, x)), down, (M128("If"), r2)]))
-                    act(nb(t + 1, 1, x), e1, ACT.Copy)
-                    act(nb(t + 1, 3, x), e2, ACT.Copy)
-            if not last:
-                add("G", "send", [nb(t + 1, 2, x), nb(t + 1, 3, x)], 1000, bytes=128 * n * 4)
-                mm(group(R("pU", 144 + c0, 144 + c1), [(M128("onef"), sm("B2", 4, 3, 4))]))
-        for x, (c0, c1) in enumerate(CHUNKS):
+                    e = R("EE", 256 * (old - 1) + l0, 256 * (old - 1) + l1)
+                    tt(e, d, ln("CUT"), ALU.mult)
+                    mm(group(d, [(M128("If"), nb(t, old, x)), (M128("If"), e)]), tag="a%d%d" % (x, old))
+                    act(nb(t + 1, new, x), d, ACT.Copy)
+        for x, (c0, c1) in enumerate(chunks):
             C = c1 - c0
-            tab = R("tab2" if last and x == 0 else "tab", 256 * c0, 256 * c1)
-            cp(IND(tab, R("O2", 4 * c0, 4 * c0 + C)), zv(t + 1, x, 1))
+            tab = R("tab2" if last and x < len(chunks) - 1 else "tab", 256 * c0, 256 * c1)
+            cp(IND(tab, R("O2", 4 * c0, 4 * c0 + C)), zv(t + 1, x, 0))
             if last:
                 dma("Y", R("yx", 256 * c0, 256 * c1), tab)
-        for x, (c0, c1) in enumerate(CHUNKS):
+            elif x == 0 and margin:
+                gcopy(R("tab", 4096, 4112), R("tab", 0, 16))
+        for x, (c0, c1) in enumerate(chunks):
             C = c1 - c0
-            pool = "pool2" if last and x == 0 else "pool"
-            cp(IND(R(pool, 1024 * x, 1024 * x + 1024), R("O2", 4 * c0 + 2 * C, 4 * c0 + 3 * C)), nb(t + 1, 1, x))
+            pool = "pool2" if last and x < len(chunks) - 1 else "pool"
+            w0 = 64 * c0 + (0 if c0 < 8 else 512)
+            cp(IND(R(pool, w0, w0 + 512 + 64 * C), R("O2", 4 * c0 + 2 * C, 4 * c0 + 3 * C)), nb(t + 1, 1, x))
             if last:
-                dma("Y", R("yl", 512 * x, 512 * x + 512), R(pool, 512 * x + 512, 512 * x + 1024))
+                dma("Y", R("yl", 64 * c0, 64 * c1), R(pool, 512 + 64 * c0, 512 + 64 * c1))
         if not last:
-            act(R("junk", 0, 16), R("pU", 144, 160), ACT.Copy, scale=1.0 / 512, accum=col(8))
-            if PS:
-                act(col(10), col(8), ACT.Identity, MAGIC, 0.4999)
-                act(col(11), col(10), ACT.Identity, 2 * MAGIC, -2.0)
-                act(col(12), col(8), ACT.Identity, col(11))
-                act(R("THR", t + 1, t + 2), col(12), ACT.Identity, R("THR", 0, 1))
-            else:
-                cp(R("ci", 4, 5), col(8))
+            pE = "pE%d" % ((len(chunks) - 1) % 2)
+            calls = []
+            for c0, c1 in chunks:
+                calls += group(R(pE, 176 + c0, 176 + c1), [(M128("onef"), R("B2", c0 + 3 * c1, 4 * c1))])
+            mm(calls, tag="count")
+            act(R("junk", 0, 16), R(pE, 176, 192), ACT.Copy, scale=1.0 / 512, accum=CNT)
+            if P["parity"] == "V":
+                cp(R("ci", 4, 5), CNT)
                 ts(R("ci", 5, 6), R("ci", 4, 5), 1, ALU.bitwise_and)
-                ts(R("THR", t + 1, t + 2), R("ci", 5, 6), R("THR", 0, 1), ALU.add)
+                ts(R("THR", t + 1, t + 2), R("ci", 5, 6), 32768.0, ALU.mult, R("THR", 0, 1), ALU.add)
+            else:
+                act(col(8), CNT, ACT.Identity, MAGIC, 0.4999)
+                act(col(9), col(8), ACT.Identity, 2 * MAGIC, -2.0)
+                act(col(10), col(9), ACT.Identity, R("THR", 0, 1), 32768.0)
+                act(R("THR", t + 1, t + 2), CNT, ACT.Identity, col(10), 32768.0)
     for x, (l0, l1) in enumerate(lanes):
         q = "S" if x == len(lanes) - 1 else "Y"
         dma(q, R("yq", l0, l1), nb(VIS, 3, x))
         dma(q, R("yc", l0, l1), nb(VIS, 1, x))
-        dma(q, R("yz", l0, l1), zv(VIS, x, 0))
+        dma(q, R("yz", l0, l1), zv(VIS, x, 1))
         dma(q, R("yp", l0, l1), nb(VIS, 0, x))
     return ops
 
@@ -447,136 +501,137 @@ def program():
 def depend(ops):
     hist = {}
     for j, op in enumerate(ops):
-        pre, raw = set(), set()
-        for a, w in [(a, False) for a in op["rd"]] + [(a, True) for a in op["wr"]]:
+        pre = set()
+        uses = [(a, False) for a in op["rd"]] + [(a, True) for a in op["wr"]]
+        for a, w in uses:
             for (lo, hi, k, kw) in hist.get(a["ref"], []):
-                if (w or kw) and lo < a["hi"] and a["lo"] < hi and k != j:
+                if (w or kw) and lo < a["hi"] and a["lo"] < hi and k != j and not (w and kw and op["acc"] and ops[k]["acc"]):
                     pre.add(k)
-                    if kw and not w:
-                        raw.add(k)
-        for a in op["wr"]:
-            hist[a["ref"]] = [e for e in hist.get(a["ref"], []) if not (a["lo"] <= e[0] and e[1] <= a["hi"] and e[2] != j)]
-        for a, w in [(a, False) for a in op["rd"]] + [(a, True) for a in op["wr"]]:
+        if not op["acc"]:
+            for a in op["wr"]:
+                if a["ix"][0] == slice(0, 128) and a["n"] == a["hi"] - a["lo"]:
+                    hist[a["ref"]] = [e for e in hist.get(a["ref"], []) if not (a["lo"] <= e[0] and e[1] <= a["hi"])]
+        for a, w in uses:
             hist.setdefault(a["ref"], []).append((a["lo"], a["hi"], j, w))
         op["pre"] = pre
-        op["own"] = {k for k in pre - raw if INORDER and ops[k]["eng"] == op["eng"] and "bytes" not in ops[k] and "bytes" not in op
-                     and not any("off" in a for a in op["wr"] + ops[k]["wr"])}
-        op["banks"] = {a["ref"] for a in op["rd"] + op["wr"] if psum(a)}
+        op["banks"] = {a["ref"] for a, w in uses if psum(a)}
 
 
-def flight(op):
-    return 0.0 if "bytes" not in op else 1900.0 + op["bytes"] / 220.0
+MODEL = {"cycle": 1.04, "gather": 1.56, "scatter": 3.8, "tensor": 0.55, "wake": 100.0, "start": 1000.0, "rate": 400.0}
 
 
-def schedule(ops, delta):
-    n = len(ops)
-    suc = [[] for _ in ops]
-    for j, op in enumerate(ops):
-        for k in op["pre"]:
-            suc[k].append(j)
-    prio = [0.0] * n
-    for j in range(n - 1, -1, -1):
-        prio[j] = ops[j]["dur"] + flight(ops[j]) + max([LAT + prio[k] for k in suc[j]] + [0.0])
-    prio = [p + delta.get(op["tag"], 0) for p, op in zip(prio, ops)]
-    left = [len(op["pre"]) for op in ops]
-    rdy = {e: [] for e in "VSPGY"}
-    at = [0.0] * n
-    for j in range(n):
-        if left[j] == 0:
-            rdy[ops[j]["eng"]].append(j)
-    free = {e: 0.0 for e in rdy}
-    bank, order, extra, fin, wire = {}, [], {}, [0.0] * n, [0.0]
-
-    def est(j):
-        s = max(at[j], free[ops[j]["eng"]])
-        for b in ops[j]["banks"]:
-            for e, k in bank.get(b, {}).items():
-                if e != ops[j]["eng"]:
-                    s = max(s, fin[k] + LAT)
-        return s
-
-    while len(order) < n:
-        best = None
-        for e, lst in rdy.items():
-            if not lst:
-                continue
-            es = {j: est(j) for j in lst}
-            t0 = min(es.values())
-            pick = None
-            for c in lst:
-                end = es[c] + ops[c]["dur"]
-                score = max([es[c] + prio[c]] + [max(es[o], end) + prio[o] for o in lst if o != c]) + IDLE * (es[c] - t0)
-                key = (score, -prio[c])
-                if pick is None or key < pick[0]:
-                    pick = (key, c)
-            c = pick[1]
-            if best is None or es[c] < best[0]:
-                best = (es[c], c)
-        s, j = best
-        op = ops[j]
-        e = op["eng"]
-        rdy[e].remove(j)
-        extra[j] = set()
-        for b in op["banks"]:
-            extra[j] |= {k for f, k in bank.get(b, {}).items() if f != e}
-            bank.setdefault(b, {})[e] = j
-        free[e] = s + op["dur"]
-        fin[j] = free[e]
-        if "bytes" in op:
-            wire[0] = max(wire[0], fin[j] + 1900.0) + op["bytes"] / 220.0
-            fin[j] = wire[0]
-        order.append(j)
-        for k in suc[j]:
-            at[k] = max(at[k], fin[j] + LAT)
-            left[k] -= 1
-            if left[k] == 0:
-                rdy[ops[k]["eng"]].append(k)
-    return order, extra, max(fin)
+def duration(op, m):
+    c = op["cost"]
+    return c[0] + m["cycle"] * (c[1] + m["gather"] * c[2] + m["scatter"] * c[3]) + m["tensor"] * c[4]
 
 
-IDLE = 1.0
+def moving(op, m):
+    if op["kind"] == "fold":
+        return 2 * op["bytes"] / m["rate"], m["start"] + op["bytes"] / m["rate"]
+    return op["bytes"] / m["rate"], 0.0
 
 
-def placed(ops):
-    place = dict(zip(sorted({op["tag"] for op in ops}), (int(v) for v in PLACE.split(","))))
-    shift = {s.split(":")[0]: int(s.split(":")[1]) for s in SHIFT.split(",") if s}
+def label(op):
+    return ("_" if op["visit"] < 0 else "") + op["tag"]
+
+
+def ranked(ops, place):
     key = []
     for op in ops:
-        k = 1000 * max(op["visit"], 0) + place[op["tag"]] + shift.get("%s@%d" % (op["tag"], op["visit"]), 0)
-        for p in sorted(op["pre"]):
+        k = 1000 * max(op["visit"], 0) + place[label(op)]
+        for p in op["pre"]:
             if key[p] >= k:
                 k = key[p] + 0.001
         key.append(k)
-    order = sorted(range(len(ops)), key=lambda j: (key[j], j))
-    return banks(ops, order)
+    return sorted(range(len(ops)), key=lambda j: key[j])
 
 
-def listed(ops):
-    digits = "0123456789abcdefghijklmnopqrstuvwxyzABCDEFGHIJKLMNOPQRSTUVWXYZ"
-    order = [62 * digits.index(ORDER[i]) + digits.index(ORDER[i + 1]) for i in range(0, len(ORDER), 2)]
-    return banks(ops, order)
+def prepare(ops, m):
+    rows = []
+    for op in ops:
+        lag = [(k, 0.0 if op["eng"] == "P" == ops[k]["eng"] else m["wake"]) for k in op["pre"]]
+        rows.append((op["eng"], duration(op, m), lag, op["banks"], moving(op, m) if "bytes" in op else None))
+    return rows, m["wake"], m["start"]
 
 
-def banks(ops, order):
-    bank, extra = {}, {}
+def gap(starts, ends, t, d):
+    lo, hi = 0, len(ends)
+    while lo < hi:
+        mid = (lo + hi) // 2
+        if ends[mid] <= t:
+            lo = mid + 1
+        else:
+            hi = mid
+    while lo < len(starts) and starts[lo] < t + d - 1e-6:
+        t = ends[lo]
+        lo += 1
+    return t, lo
+
+
+def serial(prepared, order):
+    rows, wake, start = prepared
+    begin, done = [0.0] * len(rows), [0.0] * len(rows)
+    taken = {e: ([], []) for e in "VSPGYW"}
+    bank = {}
     for j in order:
-        extra[j] = set()
-        for b in ops[j]["banks"]:
-            extra[j] |= {k for f, k in bank.get(b, {}).items() if f != ops[j]["eng"]}
-            bank.setdefault(b, {})[ops[j]["eng"]] = j
-    return order, extra, 0.0
+        e, d, lag, banks, move = rows[j]
+        t = 0.0
+        for k, w in lag:
+            if done[k] + w > t:
+                t = done[k] + w
+        starts, ends = taken[e]
+        while True:
+            t, at = gap(starts, ends, t, d)
+            t1 = t
+            for b in banks:
+                for s, f, other in bank.get(b, ())[-24:]:
+                    if other != e and s < t + d + wake - 1e-6 and t < f + wake - 1e-6:
+                        t = f + wake
+            if t == t1:
+                break
+        starts.insert(at, t)
+        ends.insert(at, t + d)
+        for b in banks:
+            bank.setdefault(b, []).append((t, t + d, e))
+        begin[j], done[j] = t, t + d
+        if move:
+            starts, ends = taken["W"]
+            t, at = gap(starts, ends, t + d + start, move[0])
+            starts.insert(at, t)
+            ends.insert(at, t + move[0])
+            done[j] = t + move[0] + move[1]
+    return begin, max(done)
 
 
-def plan():
-    ops = program()
+def plan(P):
+    ops = program(P)
     depend(ops)
-    order, extra, end = listed(ops) if ORDER else placed(ops) if PLACE else schedule(ops, DELTA)
+    place = P["place"]
+    if isinstance(place, str) and ":" not in place:
+        place = dict(zip(sorted({label(op) for op in ops}), (int(w) for w in place.split())))
+    elif isinstance(place, str):
+        place = {w.split(":")[0]: int(w.split(":")[1]) for w in place.split()}
+    place = {label(op): place.get(label(op), 0) for op in ops}
+    order = ranked(ops, place)
+    bank, closing = {}, {}
     count, names, known = {}, [], {e: {} for e in "VSPGY"}
-    for j in order:
+    for pos, j in enumerate(order):
         op = ops[j]
         e = op["eng"]
+        pre = set(op["pre"])
+        for b in op["banks"]:
+            pre |= {k for f, k in bank.get(b, {}).items() if f != e}
+            bank.setdefault(b, {})[e] = j
+        if op["kind"] == "mm":
+            for c in op["args"]:
+                rows = c[0]["ix"][0]
+                for w in [(c[0]["ref"], p) for p in range(rows.start, rows.stop, 16)]:
+                    if w in closing and not c[3]:
+                        closing[w][4] = False
+                    closing[w] = c
+                c.append(True)
         waits = {}
-        for k in sorted((op["pre"] - op["own"]) | extra[j], key=lambda k: -ops[k]["pos"]):
+        for k in sorted(pre, key=lambda k: -ops[k]["pos"]):
             sem, val = ops[k]["sig"]
             if known[e].get(sem, 0) < val and not (e == "P" and sem == "cP"):
                 waits[sem] = max(waits.get(sem, 0), val)
@@ -584,37 +639,66 @@ def plan():
                 for s, v in ops[k]["knows"].items():
                     known[e][s] = max(known[e].get(s, 0), v)
         op["waits"] = waits
-        op["pos"] = len(names) + sum(count.values())
+        op["pos"] = pos
         op["knows"] = {} if op["kind"] == "send" else dict(known[e])
-        if "bytes" in op:
+        if op["kind"] == "fold":
+            count[op["tag"]] = count.get(op["tag"], 0) + NENG * (len(op["args"]) // 3)
+            names += [] if op["tag"] in names else [op["tag"]]
+            op["sig"] = (op["tag"], count[op["tag"]])
+        elif "bytes" in op:
             names.append("d%d" % len(names))
             op["sig"] = (names[-1], NENG if op["kind"] == "send" else 16)
         else:
             count[e] = count.get(e, 0) + 1
             op["sig"] = ("c" + e, count[e])
-    return [ops[j] for j in order], names, end
+    return [ops[j] for j in order], names
 
 
-OPS, _names, ESTIMATE = plan()
+PLAN["place"] = "_Voneb0:-2978 _Ynbi0:-2959 _Ywi0:-2921 _Ynbi256:-2917 _VB240:-2657 _VTC768:-2559 _VCq0:-2506 _Ynbi512:-2378 _Gi160:-2253 _Gi2560:-2250 _SZV128:-2216 _Ypooli0:-2174 _Ytab0:-2136 _VCn0:-2129 _SZV384:-2106 _Vzero0:-2065 _Gci0:-2034 _GiB0:-2031 _GIf0:-2027 _Gonef0:-2016 _Vci2:-1997 _Gic0:-1993 _Vci1:-1970 _VCn0.2:-1884 _Gib0:-1865 _Vcf0:-1846 _Vcf3:-1831 _VSEL0:-1804 _VBM0:-1800 _VNB0:-1789 _Vcf1:-1785 _Vcf6:-1733 _Vcf4:-1714 _Gia0:-1695 _VNB256:-1642 _Stab2048:-1619 _VNB384:-1567 _VDL0:-1450 _VBM24:-1446 _VRM0:-1434 _VWb0:-1299 _VSEL8:-1295 _VTC0:-1246 _Vcf11:-1242 _Stab4096:-1193 _SInb0:-1046 _SIh0:-1008 _Sic0:-925 _YMK0:-661 _Ydi0:-653 _SI320:-593 _Vtb0:-536 _Vta0:-457 _VNB512:-442 _VNB128:-427 _VBM8:-423 _Vpool1024:-412 _VNB640:-397 _Vpool512:-348 _SInf0:-340 _VTC512:-272 _YMK2048:-151 _SIb0:-114 _VKC8:-23 _VKC24:-12 _Vcf5:18 _VBM16:26 _VKC0:33 _VB40:37 _VSEL16:45 _VD00:49 _GONE0:52 _Vcf2:86 _Gidd0:90 _VB20:94 _VB232:98 _VTHR0:109 _VSEL24:173 _Vlast0:188 _VB28:218 _VKC16:290 _GiJ0:309 _VZw0:324 raw0:-1853 u0:-1465 e1:-1280 u1:-936 VQI256:-721 SAY3072:-706 Yyc0:-699 GNB640:-650 STU0:-548 PpR0.2:-544 dc1:-540 ST1128:-533 Yyx2048:-521 PpR0:-472 Ytab20:-468 STU10:-438 e0:-416 VNU256:-408 ST1512:-404 ST10:-400 z10:-393 ST1256:-382 raw1:-370 VNU0:-359 VQS256:-351 VOFF256:-302 VNU512:-291 VQI0:-287 VQI512:-276 VQS0:-265 VQS512:-257 ST1384:-238 VOFF0:-227 SX0:-223 SDY1024:-219 VTU128:-212 VOFF512:-208 VDY0:-200 VNU384:-197 SAY3584:-189 VNU128:-185 VNU640:-182 VQI128:-178 VQI384:-170 VQS128:-167 SCUT0:-163 Yyx0:-159 ST1640:-155 VQS384:-148 VQI640:-144 VOFF128:-133 SX1024:-125 VQS640:-121 VOFF384:-117 SDY2048:-110 VOFF640:-99 SAY1024:-95 Yyq0:-91 VFK128:-87 dq1:-84 dc0:-80 VDV1024:-76 VDV2048:-72 VDV0:-68 GNB512:-57 SX2048:-53 VAV1024:-50 Yyp0:-42 VAV0:-19 SAY1536:0 SAY0:11 k1:15 dq0:56 sDV8:67 fold2:71 sDV12:101 sDV0:105 z0:113 SX3072:120 VE128:124 sAY0:128 k0:132 VUM0:158 sAV0:162 SSG0:166 VE0:177 SDY3072:184 VFK0:192 sDY8:203 VW116:207 VKX0:222 Ypool2512:226 PpR0.3:233 VEE256:237 PpR0.4:241 z11:245 VDV3072:252 VK0:256 VAV3072:260 VB224:264 VW224:271 VW10:275 VMK2048:283 VB248:298 VO10:313 sAV12:316 VK16:320 VW2s24:328 VMK0:332 Scf8:335 VO224:354 VB216:362 VMS0:366 SDI0:369 SRT0:373 sAY12:377 VNB768:384 VEE0:388 Syp128:392 sAV8:396 sAY8:400 VB256:411 VO116:415 VKX128:418 a01:422 SSG128:426 SXM0:430 um0:437 SDI128:445 SZV0:449 SZV256:471 VMS2048:475 count:483 Yyz0:486 Vtab20:490 VW20:498 VW28:501 SNB256:505 VW216:509 a02:513 um1:516 VW256:520 VW2s0:524 SXM256:539 SNB128:547 Gtab4096:569 SNB768:581 VO20:611 SXM384:615 SNB0:626 Vtab0:633 VUM8:637 VW232:645 VW240:656 Sjunk0:664 SRT256:667 VW248:671 VW2s32:675 VW2s40:679 VO232:683 VO240:686 SCUT128:690 Vtab2048:694 VNB896:716 VZV384:732 VpF10:739 Syq128:766 VpF1128:769 VNB384:796 Scf10:860 STHR0:898 Vpool20:939 YMK2048:962 Vpool1024:1060 Vpool0:1139 Yyl0:1143 YMK0:1150 Yyl512:1181 Scf9:1230 Syc128:1249 Syz128:1403"
+PLAN.update(v="GVGV", y="FMFS", whole="00", place="-115 -134 175 244 41 -653 -401 160 713 354 629 -176 -58 99 522 721 393 251 -8 431 -81 114 -375 -359 -470 -157 -447 -161 912 -600 -592 -382 -77 0 45 248 480 568 419 412 820 709 1171 667 1095 1110 1057 1954 72 225 312 -84 503 465 -203 22 -27 198 -35 213 366 343 293 217 232 229 438 15 374 255 496 286 507 793 339 755 -474 -195 -481 -149 -451 -188 -20 469 492 278 683 633 -210 -62 -275 -39 -218 -42 -237 -153 -462 -100 -249 -107 -222 -69 -420 -65 -233 -73 -214 362 576 202 450 385 377 179 595 583 587 572 381 446 240 614 610 748 770 774 1358 1080 801 557 515 729 950 828 11 -146 396 1622 1652 1221 -126 19 -791 1603 -1558 -294 -3859 -3676 -3054 -2023 -1352 -2340 -1313 -2016 -283 -2012 -394 -1119 -1165 -123 -2344 -1951 38 -1542 290 320 -1737 389 -1917 -3577 103 -3584 -321 -3855 -3523 -3298 129 -1936 -813 328 -1913 -2111 -1726 -1730 -3310 -459 -1844 -1733 -31 -3500 -1909 -184 -1932 -1970 106 -3699 -130 -1939 297 -3695 -3649 -1924 -256 -3565 -1974 -1741 -3466 -3852 -3806 -104 -4092 -191 -241 -1966 -409 -3817 -833 206 -2848 -3260 -3355 -3306 -489 -325 -3363 454 698 488 -329 3 -527 -455 -138 -516 53 309 164 427 -539 -439 133 282 125 332 137 316 -142 335 -436 118 122 7 -168 -96 -1336 -1264 370 236 404 -810 732")
+OPS, _names = plan(PLAN)
 SEMAPHORES = ["cV", "cS", "cP", "cG", "sent"] + _names
 
 
-def rank_program(g, core, T, topo):
-    rank = T.rank_of(core)
-    if rank is None:
-        return
-    nxt = T.cores[(rank + 1) % len(T.cores)]
-    rid, pid = topo.addr(nxt)[:2]
-    mask = sum(1 << e for e in topo.engines(core, nxt)[:NENG])
-    Q = {"V": g.vector, "S": g.scalar, "P": g.tensor, "G": g, "Y": g.sync}
+def helpers(T, topo):
+    pairs = {}
+    for core in T.cores:
+        spare = [c for c in topo.cores_of(core) if c not in T.cores and c not in pairs.values()]
+        pairs[core] = min(spare, key=lambda c: (topo.die(c) != topo.die(core), abs(c - core)))
+    return pairs
 
+
+def engines(topo, src, dst, half):
+    return sum(1 << e for e in topo.engines(src, dst)[NENG * half:NENG * (half + 1)])
+
+
+def rank_program(g, core, T, topo):
     def ap(a):
         if not isref(a):
             return a
         v = T[a["ref"]][a["ix"]]
         return v.indirect(ap(a["off"])) if "off" in a else v
 
-    final, sent = {}, 0
+    folds = [op for op in OPS if op["kind"] == "fold"]
+    helper = helpers(T, topo)
+    rank = T.rank_of(core)
+    if rank is None:
+        for owner, c in helper.items():
+            if c == core and folds:
+                back = DstId(rid=topo.addr(owner)[0], pnc=topo.addr(owner)[1])
+                for j, op in enumerate(folds):
+                    sem, val = op["sig"]
+                    g.wait_ge(T.sem[sem], val)
+                    g.remote_dma_fused([RemoteDMATransfer(dst_ids=[back], dma_engine_mask=engines(topo, core, owner, (i + j) % 2),
+                                                          remote_sem=T.sem[sem], src=ap(a), dst=ap(a))
+                                        for i, a in enumerate(op["args"][::3])], local_sem=T.sem.sent)
+                g.wait_ge(T.sem.sent, NENG * sum(len(op["args"]) // 3 for op in folds))
+        return
+    nxt = T.cores[(rank + 1) % len(T.cores)]
+    rid, pid = topo.addr(nxt)[:2]
+    aid = DstId(rid=topo.addr(helper[core])[0], pnc=topo.addr(helper[core])[1])
+    Q = {"V": g.vector, "S": g.scalar, "P": g.tensor, "G": g, "Y": g.sync}
+    final, sent, nf = {}, 0, 0
     for op in OPS:
         q, kind = Q[op["eng"]], op["kind"]
         for sem, val in op["waits"].items():
@@ -628,8 +712,16 @@ def rank_program(g, core, T, topo):
             continue
         a = [ap(v) for v in op["args"]]
         if kind == "send":
-            g.remote_dma(a[0], a[1], T.sem[sem], T.sem.sent, pid, rid, mask)
+            g.remote_dma_fused([RemoteDMATransfer(dst_ids=[DstId(rid=rid, pnc=pid)], dma_engine_mask=engines(topo, core, nxt, 0),
+                                                  remote_sem=T.sem[sem], srcs=[a[1], a[2]], dsts=[a[0]], alu_op=1)], local_sem=T.sem.sent)
             sent += NENG
+            continue
+        if kind == "fold":
+            g.remote_dma_fused([RemoteDMATransfer(dst_ids=[aid], dma_engine_mask=engines(topo, core, helper[core], (i // 3 + nf) % 2),
+                                                  remote_sem=T.sem[sem], srcs=[a[i + 1], a[i + 2]], dsts=[a[i]], alu_op=2)
+                                for i in range(0, len(a), 3)], local_sem=T.sem.sent)
+            sent += NENG * (len(a) // 3)
+            nf += 1
             continue
         if kind == "dma":
             whole = [T[v["ref"]][:] if v["ref"] in ("wt", "de") else w for v, w in zip(op["args"], a)]
@@ -652,8 +744,10 @@ def rank_program(g, core, T, topo):
                 ins = g.iota(a[0], a[1], a[2], a[3])
             else:
                 ins = g.iota(a[0], a[1], a[2], a[3], allow_small_or_imprecise_dtypes=True)
-        else:
+        elif a[2]:
             ins = g.affine_select(a[0], a[1], [[-1, 128]], ALU.is_equal, 0.0, 0, 1)
+        else:
+            ins = g.affine_select(a[0], a[1], [[0, op["args"][0]["n"]]], ALU.is_equal, 0.0, 0, 0)
         ins.then_inc(T.sem[sem], 1)
     g.wait_ge(T.sem.sent, sent)
     for sem, val in final.items():

from concourse.bass import DstId, RemoteDMATransfer
from concourse.mybir import AluOpType as ALU, ActivationFunctionType as ACT

VIS = 5
MAGIC = 12582912.0
NENG = 8

PLAN = {
    "chunks": [(0, 8), (8, 16)],
    "pieces": [(0, 4), (4, 8), (8, 12), (12, 16)],
    "x": "SSSS",
    "x0": "SSSS",
    "v": "VVGV",
    "y": "MSFS",
    "m": "SS",
    "u": "SV",
    "z": "SSSV",
    "parity": "S",
    "split": 1,
    "t": "JJJJJJ",
    "add": "SV",
    "early": "01",
    "apart": "01",
    "cut": "10",
    "pair": True,
    "whole": "10",
    "hbank": ["pH0"] * 3 + ["pH1"] * 3,
    "rbank": ["pR0", "pR1"],
    "place": "_Ywi0:-2026 _Voneb0:-1950 _VTC0:-1946 _Gci0:-1943 _Vci1:-1939 _VCn0:-1936 _Vci2:-1910 _VDL0:-1878 _Gic0:-1852 _GiB0:-1824 _Ynbi0:-1809 _Gonef0:-1806 _VCn0.2:-1788 _Vcf0:-1784 _Vcf4:-1762 _Ynbi512:-1751 _Gi2560:-1726 _Gi160:-1694 _Vcf2:-1650 _VWb0:-1647 _VCk0:-1643 _Vzero0:-1639 _VBM0:-1614 _Vcf3:-1600 _VNB0:-1596 _SZV128:-1560 _Ynbi256:-1528 _VCk0.2:-1524 _VB240:-1242 _VSEL8:-1239 _VNB256:-1232 _Vcf1:-1174 _VSEL0:-1170 _VBM24:-1149 _VNB512:-1145 _Vcf6:-1055 _Stab2048:-1051 _VNB128:-1040 _SI320:-863 _GIf0:-827 _Ypooli0:-802 _SInb0:-795 _Ydi0:-773 _YMK0:-741 _SZV384:-730 _Stab4096:-683 _Ytab0:-603 _Gib0:-542 _Gia0:-484 _SIb0:-477 _SIh0:-434 _VD00:-365 _VRM0:-340 _SInf0:-329 _VNB384:-322 _Vtb0:-250 _Vta0:-235 _VCq0:-224 _VSEL16:-217 _Vpool512:-210 _GiJ0:-185 _Sic0:-159 _Vpool1024:-134 _VB20:-98 _VNB640:-80 _Vcf5:-62 _VBM8:-58 _VTC512:-33 _Gidd0:-11 _VKC0:7 _VKC16:32 _VSEL24:39 _YMK2048:83 _VKC24:115 _GONE0:129 _VZw0:187 _VBM16:202 _VKC8:310 _VB232:324 _Vlast0:328 _VTHR0:339 _VB28:346 _VB40:592 _VTC768:729 STU10:-842 STN0:-777 STU0:-755 raw0:-748 hk01:-733 hp01:-578 hn01:-495 ST1512:-448 u0:-445 hp12:-380 hn02:-354 VNU256:-343 STN256:-333 hk11:-325 ST1256:-315 hn00:-300 VNU0:-297 ht01:-293 VNU512:-282 hp00:-278 ht12:-260 STN512:-213 VOFF512:-199 VKX0:-195 ST10:-188 hn10:-181 hp02:-152 raw1:-138 VOFF256:-120 SSG0:-109 ht00:-105 VTU128:-76 VDY0:-73 VNU128:-65 VOFF0:-47 hn11:-44 u1:-37 k0:-22 hp10:-19 VNU384:-15 ht02:3 a01:14 hp11:18 VTN128:21 VTN384:25 VO116:28 ht11:36 SNB768:43 ht10:46 VNU640:68 SX0:72 hn12:75 dq0:79 VOFF384:86 SX1024:93 VTN640:97 SDY1024:101 PpR0:108 Ytab20:111 VDV2048:119 e1:126 VDV0:133 PpR0.2:140 VFK128:144 z10:151 VOFF128:155 VOFF640:162 VDV1024:166 dq1:169 VAV1024:180 VAV0:184 VUM8:209 e0:220 SAY0:231 SX2048:234 VE0:241 SAY3072:256 SAY1024:281 SDY2048:288 SAY3584:292 SAY1536:296 Gtab4096:299 SDI0:303 dc1:314 Yyp0:321 SX3072:332 VEE0:335 sDV0:342 sAY0:364 sAV0:368 sDV8:371 sDY8:375 SDY3072:379 VFK0:382 dc0:393 VDV3072:407 SXM384:411 VK0:415 PpR0.3:418 PpR0.4:425 VAV3072:429 VW10:433 VB224:436 fold2:444 sDV12:447 VW224:451 sAV12:454 k1:462 VB248:465 GNB512:469 VO10:480 sAY12:483 VW116:487 VNB768:490 VB256:494 VW2s24:498 VE128:501 sAV8:509 sAY8:512 VMK0:519 Sjunk0:527 VO224:530 VMS0:534 Yyx0:537 SCUT0:541 SXM0:545 VKX128:548 SZV0:559 z0:563 SSG128:570 Yyx2048:574 Ypool2512:577 VB216:581 Scf8:584 VW216:588 um0:599 VEE256:602 VK16:606 VUM0:610 VW28:613 VW20:617 VMK2048:624 VW2s0:628 SNB256:631 SRT0:638 SXM256:642 Yyc0:649 VO20:653 SDI128:664 SNB0:682 a02:689 VMS2048:693 Yyl0:696 Scf10:711 Yyq0:714 Vtab0:725 Vpool20:732 Vtab20:736 um1:743 SRT256:747 VW256:754 VW232:779 VW248:794 VW240:797 Yyz0:808 VW2s32:823 GNB640:833 VNB896:837 SZV256:844 count:859 z11:870 VW2s40:873 VO232:877 VO240:884 Vtab2048:888 VZV384:898 SCUT128:906 VpF10:909 VpF1128:913 VNB384:916 SNB128:931 STHR0:971 Vpool1024:992 Syp128:1000 YMK2048:1104 Syc128:1263 Vpool0:1277 YMK0:1285 Scf9:1389 Syz128:1595 Yyl512:1772 Syq128:2010",
}

F, H, I, U = "float32", "bfloat16", "int32", "uint16"
SCRATCH = {
    "tab": ("sbuf", [128, 4112], H), "X": ("sbuf", [128, 4096], H), "DV": ("sbuf", [128, 4096], H),
    "DY": ("sbuf", [128, 4096], H), "AV": ("sbuf", [128, 4096], H), "AY": ("sbuf", [128, 4096], H),
    "MK": ("sbuf", [128, 4096], H), "MS": ("sbuf", [128, 4096], H), "ONE": ("sbuf", [128, 2048], H),
    "pool": ("sbuf", [128, 2048], F), "pooli": ("sbuf", [128, 1024], I), "nbi": ("sbuf", [128, 768], I),
    "tab2": ("sbuf", [128, 4096], H), "pool2": ("sbuf", [128, 2048], F),
    "ZV0": ("sbuf", [128, 512], H), "ZV1": ("sbuf", [128, 512], H),
    "OFF": ("sbuf", [128, 768], U), "NU": ("sbuf", [128, 768], F), "TN": ("sbuf", [128, 768], H),
    "QI": ("sbuf", [128, 768], I), "QS": ("sbuf", [128, 768], I), "Cj": ("sbuf", [128, 128], H),
    "T1": ("sbuf", [128, 768], F), "TU": ("sbuf", [128, 256], H), "TU1": ("sbuf", [128, 256], F),
    "SG": ("sbuf", [128, 512], F), "E": ("sbuf", [128, 512], F), "FK": ("sbuf", [128, 512], F),
    "KX": ("sbuf", [128, 512], F), "K": ("sbuf", [128, 32], I), "W1": ("sbuf", [128, 32], I),
    "O1": ("sbuf", [128, 32], U), "UM": ("sbuf", [128, 16], I), "W2": ("sbuf", [128, 64], I),
    "W2s": ("sbuf", [128, 64], F), "O2": ("sbuf", [128, 64], U), "B2": ("sbuf", [128, 64], F),
    "XM": ("sbuf", [128, 512], H), "DI": ("sbuf", [128, 256], H), "CUT": ("sbuf", [128, 256], H),
    "RT": ("sbuf", [128, 512], F), "EE": ("sbuf", [128, 512], F), "TC": ("sbuf", [128, 1280], H),
    "wi": ("sbuf", [128, 4], I), "di": ("sbuf", [128, 4], I), "ci": ("sbuf", [128, 8], I),
    "cf": ("sbuf", [128, 16], F), "THR": ("sbuf", [128, 8], F), "junk": ("sbuf", [128, 16], F),
    "iJ": ("sbuf", [128, 144], F), "iB": ("sbuf", [128, 128], F), "ia": ("sbuf", [128, 256], F),
    "ib": ("sbuf", [128, 256], F), "ic": ("sbuf", [128, 128], F), "idd": ("sbuf", [128, 128], F),
    "i16": ("sbuf", [128, 8], F), "i256": ("sbuf", [128, 8], F), "B4": ("sbuf", [128, 8], F),
    "ta": ("sbuf", [128, 256], H), "tb": ("sbuf", [128, 256], H), "last": ("sbuf", [128, 8], U),
    "BM": ("sbuf", [128, 32], F), "KC": ("sbuf", [128, 32], F), "RM": ("sbuf", [128, 128], H),
    "SEL": ("sbuf", [128, 32], H), "Wb": ("sbuf", [128, 128], H), "Zw": ("sbuf", [128, 144], H),
    "onef": ("sbuf", [128, 128], F), "If": ("sbuf", [128, 128], F), "Inf": ("sbuf", [128, 128], F),
    "I32": ("sbuf", [128, 128], F), "Ib": ("sbuf", [128, 128], H), "Inb": ("sbuf", [128, 128], H),
    "Ih": ("sbuf", [128, 128], H), "Cq": ("sbuf", [128, 128], H), "Cn": ("sbuf", [128, 128], H),
    "Ck": ("sbuf", [128, 128], H), "oneb": ("sbuf", [128, 384], H), "zero": ("sbuf", [128, 128], H),
    "D0": ("sbuf", [128, 128], F), "DL": ("sbuf", [128, 128], F),
}
for _t in range(VIS + 1):
    SCRATCH["NB%d" % _t] = ("sbuf", [128, 1024], F)
for _n in ("pE0", "pE1", "pH0", "pH1", "pF0", "pF1", "pR0", "pR1"):
    SCRATCH[_n] = ("psum", [128, 512], F)
DRAM = {"xt": H, "zt": H, "ch": I, "pa": I, "vi": I, "pl": I, "wt": I, "de": I,
        "yc": F, "yp": F, "yq": F, "yl": F, "yx": H, "yz": H}
SIZE = {F: 4, H: 2, I: 4, U: 2}


def dtype(name):
    return DRAM[name] if name in DRAM else SCRATCH[name][2]


def R(name, lo, hi, step=1, parts=(0, 128)):
    return {"ref": name, "lo": lo, "hi": hi, "n": len(range(lo, hi, step)),
            "ix": (slice(*parts), slice(lo, hi) if step == 1 else slice(lo, hi, step))}


def IND(win, off):
    return {"ref": win["ref"], "lo": win["lo"], "hi": win["hi"], "n": 16 * off["n"], "ix": win["ix"], "off": off}


def isref(a):
    return isinstance(a, dict)


def psum(a):
    return a["ref"] in SCRATCH and SCRATCH[a["ref"]][0] == "psum"


def program(P):
    ops, visit, seen = [], [-1], {}
    chunks, pieces = P["chunks"], P["pieces"]
    VIS = P.get("visits", 5)

    def add(eng, kind, args, cost, tag=None, **kw):
        rd, wr = [], []
        for call in (args if kind == "mm" else [args]):
            for j, a in enumerate(call):
                if isref(a):
                    (wr if j == 0 else rd).append(a)
                    if "off" in a:
                        rd.append(a["off"])
        if kw.get("accum") is not None:
            wr.append(kw["accum"])
        op = {"eng": eng, "kind": kind, "args": args, "cost": cost, "rd": rd, "wr": wr, "acc": False}
        op.update(kw)
        name = wr[0]["ref"]
        name = name[:2] if name[:2] in ("NB", "ZV", "pR") else name
        base = tag or "%s%s%d" % (eng, name, 0 if name == "THR" else wr[0]["lo"])
        seen[(visit[0], base)] = seen.get((visit[0], base), 0) + 1
        op["tag"] = base if seen[(visit[0], base)] == 1 else "%s.%d" % (base, seen[(visit[0], base)])
        op["visit"] = visit[0]
        ops.append(op)
        return op

    def cost(out, ins, two=False):
        if "off" in out:
            return (50, 0, 0, out["n"], 0)
        if "off" in ins[0]:
            return (50, 0, ins[0]["n"], 0, 0)
        f = 0.5 if all(SIZE[dtype(a["ref"])] == 2 for a in [out] + ins) else 1.0
        if two:
            f = 1.0 if any(psum(a) for a in ins) else 2.0
        return (30, max(64, f * out["n"]), 0, 0, 0)

    def cp(out, a):
        add("V", "cp", [out, a], cost(out, [a]))

    def tt(out, a, b, op):
        add("V", "tt", [out, a, b, op], cost(out, [a, b], True))

    def ts(out, a, s1, op0, s2=None, op1=None):
        add("V", "ts", [out, a, s1, s2, op0, op1], cost(out, [a]))

    def scan(out, a, b, op0, op1):
        add("V", "scan", [out, a, b, op0, op1], cost(out, [a, b]))

    def ms(out, v):
        add("V", "ms", [out, v], cost(out, [out]))

    def act(out, a, fn, bias=0.0, scale=1.0, accum=None):
        c = (65, 0, a["n"], 0, 0) if "off" in a else (40, max(64, a["n"]), 0, 0, 0)
        add("S", "act", [out, a, fn, bias, scale], c, accum=accum)

    def mm(calls, tag=None, acc=False, opens=False):
        cyc = sum(max(min(64, c[1]["n"]), c[0]["n"]) * (4 if dtype(c[1]["ref"]) == F else 1) for c in calls)
        op = add("P", "mm", [list(c) for c in calls], (40, 0, 0, 0, cyc), tag=tag, acc=acc)
        if opens:
            op["wr"].append(R(calls[0][0]["ref"], 0, 512))

    def group(out, pairs, start=True):
        return [(out, a, b, start and j == 0) for j, (a, b) in enumerate(pairs)]

    def iota(out, pattern, base, cm):
        add("G", "iota", [out, pattern, base, cm], (130, 2 * out["n"], 0, 0, 0))

    def gcopy(out, a, diagonal=False):
        add("G", "sel", [out, a, diagonal], (170, 2 * out["n"], 0, 0, 0))

    def dma(q, out, a):
        add(q, "dma", [out, a], (60, 0, 0, 0, 0), bytes=128 * out["n"] * SIZE[dtype(out["ref"])])

    def gather(eng, out, src):
        if eng == "V":
            cp(out, src)
        else:
            act(out, src, ACT.Copy)

    def rounded(eng, out, src, unit, tmp):
        if eng == "V":
            ts(out, src, unit * MAGIC, ALU.add, unit * MAGIC, ALU.subtract)
        else:
            act(tmp, src, ACT.Identity, MAGIC, 1.0 / unit)
            act(out, tmp, ACT.Identity, -unit * MAGIC, float(unit))

    col = lambda j: R("cf", j, j + 1)
    G16, KF, C16, C4, WF, K0, K1, CNT = (col(j) for j in range(8))
    CN = col(11)
    M128 = lambda name: R(name, 0, 128)
    low = lambda name, n: R(name, 0, n, parts=(0, 64))
    lanes = [(16 * a, 16 * b) for a, b in chunks]
    SELECT = {1: R("SEL", 0, 8), -1: R("SEL", 8, 16), 2: R("SEL", 16, 24), -2: R("SEL", 24, 32)}

    def zv(t, x, part):
        l0, l1 = lanes[x]
        n = l1 - l0
        return R("ZV%d" % (t % 2), 2 * l0 + part * n, 2 * l0 + (part + 1) * n)

    def nb(t, s, x):
        return R("NB%d" % t, 256 * s + lanes[x][0], 256 * s + lanes[x][1])

    dma("Y", R("wi", 0, 1), R("wt", 0, 1))
    for x, (l0, l1) in enumerate(lanes):
        dma("S", zv(0, x, 1), R("zt", l0, l1))
    dma("Y", R("nbi", 256, 512), R("ch", 0, 256))
    dma("Y", R("tab", 0, 2048), R("xt", 0, 2048))
    dma("S", R("tab", 2048, 4096), R("xt", 2048, 4096))
    margin = 16 if set("SV") & set(P["t"]) else 0
    if margin:
        dma("S", R("tab", 4096, 4112), R("xt", 0, 16))
    dma("Y", R("nbi", 512, 768), R("vi", 0, 256))
    dma("Y", R("nbi", 0, 256), R("pa", 0, 256))
    dma("Y", R("di", 0, 1), R("de", 0, 1))
    dma("Y", R("pooli", 0, 1024), R("pl", 0, 1024))
    iota(R("ci", 0, 1), [[0, 1]], 0, 1)
    iota(M128("iB"), [[16, 8], [0, 16]], 0, 0)
    iota(M128("ic"), [[0, 8], [1, 16]], 0, 0)
    for name, base, users in (("Ck", -6144.0, "SV"), ("Cj", -8192.0, "I")):
        if set(users) & set(P["t"]):
            ts(R(name, 0, 128, parts=(0, 32)), R("ic", 0, 128, parts=(0, 32)), 32.0, ALU.mult, base, ALU.add)
            ts(R(name, 0, 128, parts=(32, 64)), R("ic", 0, 128, parts=(32, 64)), 5.0, ALU.mult)
    iota(M128("onef"), [[0, 128]], 1, 0)
    gcopy(M128("If"), M128("onef"), True)
    iota(R("i16", 0, 8), [[16, 8]], 0, 0)
    iota(R("i256", 0, 8), [[256, 8]], 0, 0)
    iota(R("iJ", 0, 144), [[1, 144]], -15, 0)
    iota(M128("idd"), [[32, 8], [0, 16]], 1, 0)
    iota(R("ia", 0, 256), [[0, 16], [1, 16]], 0, 0)
    iota(R("ib", 0, 256), [[-1, 16], [0, 16]], 15, 0)
    iota(R("ONE", 0, 2048), [[0, 2048]], 1, 0)
    ts(R("ci", 1, 2), R("ci", 0, 1), 112, ALU.bitwise_and)
    ts(R("ci", 2, 3), R("ci", 0, 1), 15, ALU.bitwise_and)
    cp(G16, R("ci", 1, 2))
    cp(KF, R("ci", 2, 3))
    ts(C16, R("ci", 2, 3), 16.0, ALU.mult)
    ts(C4, R("ci", 2, 3), 4.0, ALU.mult)
    ts(K0, R("ci", 1, 2), -65536.0, ALU.mult)
    ts(K1, R("ci", 1, 2), 4096.0, ALU.mult, 2048.0 * 18 + 15 + 15 / 32, ALU.add)
    if "J" in P["t"]:
        ts(CN, R("ci", 2, 3), 1184.0, ALU.mult, -262144.0, ALU.add)
    cp(WF, R("wi", 0, 1))
    ts(R("THR", 0, 1), R("di", 0, 1), 1.0, ALU.add, 32768.0, ALU.mult)
    ts(M128("Wb"), M128("iB"), G16, ALU.is_equal, WF, ALU.mult)
    ms(R("Cn", 0, 128, parts=(0, 32)), -64.0)
    ms(R("Cn", 0, 128, parts=(32, 64)), 1.0 / 64)
    ms(R("oneb", 0, 384), 1.0)
    ms(low("Cq", 128), -1.0 / 256)
    ms(M128("zero"), 0.0)
    for name, s in (("Inb", -1.0), ("I32", 32.0), ("Ib", 1.0), ("Inf", -1.0), ("Ih", 0.5)):
        if name != "I32" or set("SVI") & set(P["t"]):
            act(M128(name), M128("If"), ACT.Copy, scale=s)
    for s, a in SELECT.items():
        ts(a, R("i16", 0, 8), G16, ALU.is_equal, float(s), ALU.mult)
    ts(R("Zw", 0, 144), R("iJ", 0, 144), G16, ALU.is_equal, WF, ALU.mult)
    ts(M128("RM"), M128("ic"), KF, ALU.is_equal)
    act(M128("ic"), M128("ic"), ACT.Copy, scale=1.0 / 32768)
    tt(M128("D0"), M128("ic"), M128("idd"), ALU.add)
    ms(M128("DL"), 16.0 / 32768)
    ts(R("last", 0, 8), R("i16", 0, 8), 15.0, ALU.add)
    ts(R("B4", 0, 8), R("i256", 0, 8), 0.25, ALU.mult, C4, ALU.add)
    for x, (c0, c1) in enumerate(chunks):
        C = c1 - c0
        ts(R("BM", 2 * c0, 2 * c0 + C), R("i16", 0, C), G16, ALU.is_equal, 32768.0, ALU.mult)
        ts(R("BM", 2 * c0 + C, 2 * c1), R("i16", 0, C), G16, ALU.is_equal, -2048.0, ALU.mult)
        ts(R("KC", 2 * c0, 2 * c0 + C), R("i256", 0, C), K0, ALU.add)
        ts(R("KC", 2 * c0 + C, 2 * c1), R("i256", 0, C), K1, ALU.add)
        ts(R("B2", 4 * c0, 4 * c0 + C), R("i256", 0, C), C16, ALU.add)
        ms(R("B2", 4 * c0 + C, 4 * c0 + 2 * C), 0.0)
        dma("Y", R("MK", 256 * c0, 256 * c1), R("ONE", 0, 256 * C))
        if C < 8:
            ms(R("FK", 128 * x, 128 * x + 128), 0.0)
    ms(R("TC", 0, 512), 0.0)
    ms(R("TC", 768, 1280), 0.0)
    ts(R("ta", 0, 256), R("ia", 0, 256), KF, ALU.is_le)
    ts(R("tb", 0, 256), R("ib", 0, 256), KF, ALU.is_ge)
    tt(R("TC", 512, 768), R("ta", 0, 256), R("tb", 0, 256), ALU.mult)
    for x, (l0, l1) in enumerate(lanes):
        for s in (1, 2, 0):
            cp(nb(0, s, x), R("nbi", 256 * s + l0, 256 * s + l1))
    for j in range(2):
        cp(R("pool", 512 * j + 512, 512 * j + 1024), R("pooli", 512 * j, 512 * j + 512))

    TAB = R("tab", 0, 4096 + margin)
    nr = [0]
    for t in range(VIS):
        last = t == VIS - 1
        visit[0] = t
        if last:
            c = chunks[-1][0]
            dma("Y", R("tab2", 0, 256 * c), R("tab", 0, 256 * c))
            dma("Y", R("pool2", 512, 512 + 64 * c), R("pool", 512, 512 + 64 * c))
        for x, (l0, l1) in enumerate(lanes):
            n = l1 - l0
            pE = "pE%d" % (x % 2)
            z, raw, u, tu = zv(t, x, 1), R(pE, 256, 256 + n), R(pE, 384, 384 + n), R("TU", l0, l1)
            mm(group(raw, [(low("Cn", 128), low("oneb", n)), (M128("Wb"), z)]), tag="raw%d" % x)
            rounded(P["u"][x], tu, raw, 4096, R("TU1", l0, l1))
            mm(group(u, [(M128("Wb"), z), (M128("Inb"), tu)]), tag="u%d" % x)
            for s in (1, 2, 0):
                a, b = 256 * s + l0, 256 * s + l1
                Q, how = R(P["hbank"][3 * x + s], s * n, s * n + n), P["t"][3 * x + s]
                tt(R("NU", a, b), nb(t, s, x), u, ALU.mult)
                if how in "IJ":
                    if how == "I":
                        mm(group(Q, [(low("Cj", 128), low("oneb", n)), (M128("I32"), nb(t, s, x))]), tag="hn%d%d" % (x, s))
                    else:
                        act(R("T1", a, b), nb(t, s, x), ACT.Identity, CN, 32.0)
                        ops[-2]["args"][0] = ops[-2]["wr"][0] = Q
                    tt(R("QI", a, b), R("NU" if how == "I" else "T1", a, b), Q, ALU.add)
                    ts(R("QS", a, b), R("QI", a, b), 5, ALU.arith_shift_right, 4095, ALU.bitwise_and)
                    cp(R("OFF", a, b), R("QS", a, b))
                else:
                    terms = [(low("Ck", 128), low("oneb", n)), (M128("I32"), nb(t, s, x)), (M128("If"), R("NU", a, b))]
                    mm(group(Q, terms), tag="hp%d%d" % (x, s))
                    rounded(how, R("TN", a, b), Q, 131072, R("T1", a, b))
                    mm(group(Q, terms + [(M128("Inb"), R("TN", a, b))]), tag="ht%d%d" % (x, s))
                    ts(R("OFF", a, b), Q, 1.0 / 32, ALU.mult, 2048 - 31 / 64, ALU.add)
        for x, (c0, c1) in enumerate(chunks):
            n = 16 * (c1 - c0)
            pE = "pE%d" % (x % 2)
            mine = [pc for pc, (a, b) in enumerate(pieces) if c0 <= a < c1]
            mm(group(R(pE, 0, 128), [(low("zero", 128), low("oneb", 128))]), tag="e%d" % x, opens=True)

            def sums(name, a, b, w):
                at = (16 * (a - c0), 16 * (b - c0))
                for j in range(P["split"]):
                    mm([(R(pE, k, 128, 16, parts=at), R(name, 256 * a + k, 256 * b, 16), SELECT[w], False)
                        for k in range(j, 16, P["split"])], tag="s%s%d" % (name, a), acc=True)

            for pc in mine:
                a, b = pieces[pc]
                gather(P["x" if t else "x0"][pc], R("X", 256 * a, 256 * b), IND(TAB, R("OFF", 256 + 16 * a, 256 + 16 * b)))
            for s, key, dn, an, w in ((2, "v", "DV", "AV", 1), (0, "y", "DY", "AY", -1)):
                for pc in mine:
                    a, b = pieces[pc]
                    big = lambda name, u=a, v=b: R(name, 256 * u, 256 * v)
                    src, route = IND(TAB, R("OFF", 256 * s + 16 * a, 256 * s + 16 * b)), P[key][pc]
                    if route in "VM":
                        tt(big(dn), src, big("X"), ALU.subtract)
                        if route == "V":
                            ts(big(an), big(dn), 0.0, ALU.max, 2.0, ALU.mult)
                        else:
                            act(big(an), big(dn), ACT.Abs)
                    elif route == "S":
                        gather("S", big(dn), src)
                        for u in range(a, b, 2):
                            v = min(u + 2, b)
                            pr = R(P["rbank"][nr[0] % len(P["rbank"])], 0, 256 * (v - u))
                            nr[0] += 1
                            mm(group(pr, [(M128("Inb"), big("X", u, v)), (M128("Ib"), big(dn, u, v))]))
                            act(big(an, u, v), pr, ACT.Abs)
                    else:
                        gather("S" if route == "F" else "V", big(dn), src)
                        both = P["pair"] and P["v"][pc] in "FG" and P["y"][pc] in "FG"
                        if not both:
                            add("G", "fold", [big(an), big("X"), big(dn)], (1000, 0, 0, 0, 0), tag="fold%s%d" % (key, pc),
                                bytes=128 * 512 * (b - a))
            for pc in mine:
                if P["pair"] and P["v"][pc] in "FG" and P["y"][pc] in "FG":
                    a, b = pieces[pc]
                    big = lambda name: R(name, 256 * a, 256 * b)
                    op = add("G", "fold", [big("AV"), big("X"), big("DV"), big("AY"), big("X"), big("DY")], (1000, 0, 0, 0, 0),
                             tag="fold%d" % pc, bytes=128 * 1024 * (b - a))
                    op["wr"].append(op["rd"].pop(2))
            for s, key, dn, an, w in ((2, "v", "DV", "AV", 1), (0, "y", "DY", "AY", -1)):
                runs = []
                for pc in mine:
                    kind = {"V": "V", "M": "A", "S": "A", "F": "F", "G": "F"}[P[key][pc]]
                    if runs and runs[-1][0] == kind and P["whole"][x] == "1":
                        runs[-1][2] = pieces[pc][1]
                    else:
                        runs.append([kind, pieces[pc][0], pieces[pc][1]])
                for kind, a, b in runs:
                    if kind != "A":
                        sums(dn, a, b, -w)
                    if kind == "F":
                        sums(an, a, b, 2 * w)
                if all(r[0] != "F" for r in runs) and P["whole"][x] == "1":
                    sums(an, c0, c1, w)
                else:
                    for kind, a, b in runs:
                        if kind != "F":
                            sums(an, a, b, w)
            for pc in mine:
                fv, fy = P["v"][pc] in "FG", P["y"][pc] in "FG"
                if fv != fy:
                    sums("X", pieces[pc][0], pieces[pc][1], -1 if fv else 1)
            adds = [op for op in ops if op["acc"] and op["visit"] == t and op["wr"][0]["ref"] == pE]
            wide = [op for op in adds if op["wr"][0]["ix"][0] == slice(0, n)]
            if wide and len(wide) < len(adds):
                for op in wide[-P["split"]:]:
                    ops.remove(op)
                    ops.append(op)
                    op["acc"] = False
            act(R("SG", 128 * x, 128 * x + 128, parts=(0, n)), R(pE, 0, 128, parts=(0, n)), ACT.Sign, scale=-1.0)
        for x, (c0, c1) in enumerate(chunks):
            C = c1 - c0
            l0, l1 = lanes[x]
            n = l1 - l0
            pE, pF = "pE%d" % (x % 2), "pF%d" % (x % 2)
            ln = lambda name: R(name, l0, l1)
            el = lambda name: R(name, 128 * x, 128 * x + 128, parts=(0, n))
            sm = lambda name, w=1, p0=0, p1=None: R(name, w * c0 + p0 * C, w * c0 + (w if p1 is None else p1) * C)
            big = lambda name: R(name, 256 * c0, 256 * c1)
            first = c0 < 8
            oi, xi, m = sm("O1", 2, 0, 1), R("XM", 2 * l0, 2 * l0 + n), R("XM", 2 * l0 + n, 2 * l1)
            scan(el("E"), R("D0", 0, 128, parts=(0, n)), el("SG"), ALU.max, ALU.add)
            scan(el("FK"), R("DL", 0, 128, parts=(0, n)), el("E"), ALU.add, ALU.max)
            tt(R("KX", 128 * x, 128 * x + 128), IND(R("FK", 128 * x, 128 * x + 128), R("last", 0, 8)), M128("RM"), ALU.mult)
            pk = R(pE, 128, 128 + 2 * C)
            mm(group(pk, [(el("KX"), R("BM", 2 * c0, 2 * c1, parts=(0, n)))]), tag="k%d" % x)
            tt(sm("K", 2), pk, sm("KC", 2), ALU.add)
            ts(sm("W1", 2), sm("K", 2), 0x70F, ALU.bitwise_and)
            ts(sm("O1", 2), sm("W1", 2), C16, ALU.add)
            cp(IND(big("MK"), oi), R("zero", 0, n))
            scan(big("MS"), big("MK"), big("X"), ALU.mult, ALU.max)
            if not last:
                dma("Y", big("MK"), R("ONE", 0, 256 * C))
            ts(sm("W2", 4, 3, 4), sm("K", 2, 0, 1), 255, ALU.bitwise_and)
            ts(sm("B2", 4, 3, 4), sm("K", 2, 0, 1), R("THR", t, t + 1), ALU.is_ge if first else ALU.is_lt, 512.0, ALU.mult)
            tt(sm("B2", 4, 2, 3), sm("B2", 4, 3, 4), R("B4", 0, C), ALU.add)
            gather("S", ln("DI"), IND(big("DV"), oi))
            if P["apart"][x] == "1":
                gather("S", xi, IND(big("X"), oi))
                gather(P["m"][x], m, IND(big("MS"), sm("O1", 2, 1, 2)))
            else:
                gather(P["m"][x], R("XM", 2 * l0, 2 * l1), IND(big("MS"), sm("O1", 2)))
            um = R(pE, 160, 160 + C)
            mm(group(um, [(R("Zw", 15 - r, 143 - r), R("XM", m["lo"] + r, m["hi"], 16)) for r in range(16)]), tag="um%d" % x)
            quarter = (low("Cq", 128), low("oneb", n))
            calls = group(R(pF, 256, 256 + n), [quarter, (M128("Ih"), ln("DI"))])
            for pc, (a, b) in enumerate(pieces):
                if c0 <= a < c1:
                    u, v = 16 * (a - c0), 16 * (b - c0)
                    calls += group(R(pF, 256 + u, 256 + v), [(M128("Ib" if P["v"][pc] in "VM" else "Ih"), R("XM", 2 * l0 + u, 2 * l0 + v))], False)
            marks = group(R(pF, 256 + n, 256 + 2 * n), [quarter, (M128("Ih"), zv(t, x, 1)), (M128("Ih"), m)])
            if P["apart"][x] == "1":
                for j, part in enumerate((calls, marks)):
                    mm(part, tag="z%d%d" % (x, j))
                    rounded(P["z"][2 * x + j], zv(t + 1, x, j), R(pF, 256 + j * n, 256 + j * n + n), 1, R("RT", 2 * l0 + j * n, 2 * l0 + j * n + n))
            else:
                mm(calls + marks, tag="z%d" % x)
                rounded(P["z"][2 * x], R("ZV%d" % ((t + 1) % 2), 2 * l0, 2 * l1), R(pF, 256, 256 + 2 * n), 1, R("RT", 2 * l0, 2 * l1))
            cp(sm("UM"), um)
            for j, bits in enumerate((15, 1023, 3)):
                ts(sm("W2", 4, j, j + 1), sm("UM"), bits, ALU.bitwise_and)
            cuts = [0] + [1] * (P["early"][x] == "1") + [3] * (P["cut"][x] == "1") + [4]
            for p0, p1 in zip(cuts[:-1], cuts[1:]):
                tt(sm("W2s", 4, p0, p1), sm("W2", 4, p0, p1), sm("B2", 4, p0, p1), ALU.add)
                cp(sm("O2", 4, p0, p1), sm("W2s", 4, p0, p1))
            gather("S", ln("CUT"), IND(R("TC", 0, 768) if first else R("TC", 512, 1280), sm("O2", 4, 3, 4)))
            gather("S", nb(t + 1, 0, x), IND(R("pool", 512, 1536), sm("O2", 4, 1, 2)))
            d1, d2 = R(pF, 0, n), R(pF, 128, 128 + n)
            mm(group(d1, [(M128("If"), nb(t, 0, x)), (M128("Inf"), nb(t, 1, x))]), tag="dc%d" % x)
            mm(group(d2, [(M128("If"), nb(t, 1, x)), (M128("Inf"), nb(t, 2, x))]), tag="dq%d" % x)
            for d, old, new in ((d2, 2, 3), (d1, 1, 1)):
                if old == 2 and not last:
                    tt(nb(t + 1, 3, x), d, ln("CUT"), ALU.mult)
                    add("G", "send", [nb(t + 1, 2, x), nb(t + 1, 3, x), nb(t, 2, x)], (1000, 0, 0, 0, 0), bytes=128 * n * 8)
                elif P["add"][x] == "V":
                    tt(d, d, ln("CUT"), ALU.mult)
                    tt(nb(t + 1, new, x), d, nb(t, old, x), ALU.add)
                else:
                    e = R("EE", 256 * (old - 1) + l0, 256 * (old - 1) + l1)
                    tt(e, d, ln("CUT"), ALU.mult)
                    mm(group(d, [(M128("If"), nb(t, old, x)), (M128("If"), e)]), tag="a%d%d" % (x, old))
                    act(nb(t + 1, new, x), d, ACT.Copy)
        for x, (c0, c1) in enumerate(chunks):
            C = c1 - c0
            tab = R("tab2" if last and x < len(chunks) - 1 else "tab", 256 * c0, 256 * c1)
            cp(IND(tab, R("O2", 4 * c0, 4 * c0 + C)), zv(t + 1, x, 0))
            if last:
                dma("Y", R("yx", 256 * c0, 256 * c1), tab)
            elif x == 0 and margin:
                gcopy(R("tab", 4096, 4112), R("tab", 0, 16))
        for x, (c0, c1) in enumerate(chunks):
            C = c1 - c0
            pool = "pool2" if last and x < len(chunks) - 1 else "pool"
            w0 = 64 * c0 + (0 if c0 < 8 else 512)
            cp(IND(R(pool, w0, w0 + 512 + 64 * C), R("O2", 4 * c0 + 2 * C, 4 * c0 + 3 * C)), nb(t + 1, 1, x))
            if last:
                dma("Y", R("yl", 64 * c0, 64 * c1), R(pool, 512 + 64 * c0, 512 + 64 * c1))
        if not last:
            pE = "pE%d" % ((len(chunks) - 1) % 2)
            calls = []
            for c0, c1 in chunks:
                calls += group(R(pE, 176 + c0, 176 + c1), [(M128("onef"), R("B2", c0 + 3 * c1, 4 * c1))])
            mm(calls, tag="count")
            act(R("junk", 0, 16), R(pE, 176, 192), ACT.Copy, scale=1.0 / 512, accum=CNT)
            if P["parity"] == "V":
                cp(R("ci", 4, 5), CNT)
                ts(R("ci", 5, 6), R("ci", 4, 5), 1, ALU.bitwise_and)
                ts(R("THR", t + 1, t + 2), R("ci", 5, 6), 32768.0, ALU.mult, R("THR", 0, 1), ALU.add)
            else:
                act(col(8), CNT, ACT.Identity, MAGIC, 0.4999)
                act(col(9), col(8), ACT.Identity, 2 * MAGIC, -2.0)
                act(col(10), col(9), ACT.Identity, R("THR", 0, 1), 32768.0)
                act(R("THR", t + 1, t + 2), CNT, ACT.Identity, col(10), 32768.0)
    for x, (l0, l1) in enumerate(lanes):
        q = "S" if x == len(lanes) - 1 else "Y"
        dma(q, R("yq", l0, l1), nb(VIS, 3, x))
        dma(q, R("yc", l0, l1), nb(VIS, 1, x))
        dma(q, R("yz", l0, l1), zv(VIS, x, 1))
        dma(q, R("yp", l0, l1), nb(VIS, 0, x))
    return ops


def depend(ops):
    hist = {}
    for j, op in enumerate(ops):
        pre = set()
        uses = [(a, False) for a in op["rd"]] + [(a, True) for a in op["wr"]]
        for a, w in uses:
            for (lo, hi, k, kw) in hist.get(a["ref"], []):
                if (w or kw) and lo < a["hi"] and a["lo"] < hi and k != j and not (w and kw and op["acc"] and ops[k]["acc"]):
                    pre.add(k)
        if not op["acc"]:
            for a in op["wr"]:
                if a["ix"][0] == slice(0, 128) and a["n"] == a["hi"] - a["lo"]:
                    hist[a["ref"]] = [e for e in hist.get(a["ref"], []) if not (a["lo"] <= e[0] and e[1] <= a["hi"])]
        for a, w in uses:
            hist.setdefault(a["ref"], []).append((a["lo"], a["hi"], j, w))
        op["pre"] = pre
        op["banks"] = {a["ref"] for a, w in uses if psum(a)}


MODEL = {"cycle": 1.04, "gather": 1.56, "scatter": 3.8, "tensor": 0.55, "wake": 100.0, "start": 1000.0, "rate": 400.0}


def duration(op, m):
    c = op["cost"]
    return c[0] + m["cycle"] * (c[1] + m["gather"] * c[2] + m["scatter"] * c[3]) + m["tensor"] * c[4]


def moving(op, m):
    if op["kind"] == "fold":
        return 2 * op["bytes"] / m["rate"], m["start"] + op["bytes"] / m["rate"]
    return op["bytes"] / m["rate"], 0.0


def label(op):
    return ("_" if op["visit"] < 0 else "") + op["tag"]


def ranked(ops, place):
    key = []
    for op in ops:
        k = 1000 * max(op["visit"], 0) + place[label(op)]
        for p in op["pre"]:
            if key[p] >= k:
                k = key[p] + 0.001
        key.append(k)
    return sorted(range(len(ops)), key=lambda j: key[j])


def prepare(ops, m):
    rows = []
    for op in ops:
        lag = [(k, 0.0 if op["eng"] == "P" == ops[k]["eng"] else m["wake"]) for k in op["pre"]]
        rows.append((op["eng"], duration(op, m), lag, op["banks"], moving(op, m) if "bytes" in op else None))
    return rows, m["wake"], m["start"]


def gap(starts, ends, t, d):
    lo, hi = 0, len(ends)
    while lo < hi:
        mid = (lo + hi) // 2
        if ends[mid] <= t:
            lo = mid + 1
        else:
            hi = mid
    while lo < len(starts) and starts[lo] < t + d - 1e-6:
        t = ends[lo]
        lo += 1
    return t, lo


def serial(prepared, order):
    rows, wake, start = prepared
    begin, done = [0.0] * len(rows), [0.0] * len(rows)
    taken = {e: ([], []) for e in "VSPGYW"}
    bank = {}
    for j in order:
        e, d, lag, banks, move = rows[j]
        t = 0.0
        for k, w in lag:
            if done[k] + w > t:
                t = done[k] + w
        starts, ends = taken[e]
        while True:
            t, at = gap(starts, ends, t, d)
            t1 = t
            for b in banks:
                for s, f, other in bank.get(b, ())[-24:]:
                    if other != e and s < t + d + wake - 1e-6 and t < f + wake - 1e-6:
                        t = f + wake
            if t == t1:
                break
        starts.insert(at, t)
        ends.insert(at, t + d)
        for b in banks:
            bank.setdefault(b, []).append((t, t + d, e))
        begin[j], done[j] = t, t + d
        if move:
            starts, ends = taken["W"]
            t, at = gap(starts, ends, t + d + start, move[0])
            starts.insert(at, t)
            ends.insert(at, t + move[0])
            done[j] = t + move[0] + move[1]
    return begin, max(done)


def plan(P):
    ops = program(P)
    depend(ops)
    place = P["place"]
    if isinstance(place, str) and ":" not in place:
        place = dict(zip(sorted({label(op) for op in ops}), (int(w) for w in place.split())))
    elif isinstance(place, str):
        place = {w.split(":")[0]: int(w.split(":")[1]) for w in place.split()}
    place = {label(op): place.get(label(op), 0) for op in ops}
    order = ranked(ops, place)
    bank, closing = {}, {}
    count, names, known = {}, [], {e: {} for e in "VSPGY"}
    for pos, j in enumerate(order):
        op = ops[j]
        e = op["eng"]
        pre = set(op["pre"])
        for b in op["banks"]:
            pre |= {k for f, k in bank.get(b, {}).items() if f != e}
            bank.setdefault(b, {})[e] = j
        if op["kind"] == "mm":
            for c in op["args"]:
                rows = c[0]["ix"][0]
                for w in [(c[0]["ref"], p) for p in range(rows.start, rows.stop, 16)]:
                    if w in closing and not c[3]:
                        closing[w][4] = False
                    closing[w] = c
                c.append(True)
        waits = {}
        for k in sorted(pre, key=lambda k: -ops[k]["pos"]):
            sem, val = ops[k]["sig"]
            if known[e].get(sem, 0) < val and not (e == "P" and sem == "cP"):
                waits[sem] = max(waits.get(sem, 0), val)
                known[e][sem] = val
                for s, v in ops[k]["knows"].items():
                    known[e][s] = max(known[e].get(s, 0), v)
        op["waits"] = waits
        op["pos"] = pos
        op["knows"] = {} if op["kind"] == "send" else dict(known[e])
        if op["kind"] == "fold":
            count[op["tag"]] = count.get(op["tag"], 0) + NENG * (len(op["args"]) // 3)
            names += [] if op["tag"] in names else [op["tag"]]
            op["sig"] = (op["tag"], count[op["tag"]])
        elif "bytes" in op:
            names.append("d%d" % len(names))
            op["sig"] = (names[-1], NENG if op["kind"] == "send" else 16)
        else:
            count[e] = count.get(e, 0) + 1
            op["sig"] = ("c" + e, count[e])
    return [ops[j] for j in order], names


PLAN["place"] = "_Voneb0:-2978 _Ynbi0:-2959 _Ywi0:-2921 _Ynbi256:-2917 _VB240:-2657 _VTC768:-2559 _VCq0:-2506 _Ynbi512:-2378 _Gi160:-2253 _Gi2560:-2250 _SZV128:-2216 _Ypooli0:-2174 _Ytab0:-2136 _VCn0:-2129 _SZV384:-2106 _Vzero0:-2065 _Gci0:-2034 _GiB0:-2031 _GIf0:-2027 _Gonef0:-2016 _Vci2:-1997 _Gic0:-1993 _Vci1:-1970 _VCn0.2:-1884 _Gib0:-1865 _Vcf0:-1846 _Vcf3:-1831 _VSEL0:-1804 _VBM0:-1800 _VNB0:-1789 _Vcf1:-1785 _Vcf6:-1733 _Vcf4:-1714 _Gia0:-1695 _VNB256:-1642 _Stab2048:-1619 _VNB384:-1567 _VDL0:-1450 _VBM24:-1446 _VRM0:-1434 _VWb0:-1299 _VSEL8:-1295 _VTC0:-1246 _Vcf11:-1242 _Stab4096:-1193 _SInb0:-1046 _SIh0:-1008 _Sic0:-925 _YMK0:-661 _Ydi0:-653 _SI320:-593 _Vtb0:-536 _Vta0:-457 _VNB512:-442 _VNB128:-427 _VBM8:-423 _Vpool1024:-412 _VNB640:-397 _Vpool512:-348 _SInf0:-340 _VTC512:-272 _YMK2048:-151 _SIb0:-114 _VKC8:-23 _VKC24:-12 _Vcf5:18 _VBM16:26 _VKC0:33 _VB40:37 _VSEL16:45 _VD00:49 _GONE0:52 _Vcf2:86 _Gidd0:90 _VB20:94 _VB232:98 _VTHR0:109 _VSEL24:173 _Vlast0:188 _VB28:218 _VKC16:290 _GiJ0:309 _VZw0:324 raw0:-1853 u0:-1465 e1:-1280 u1:-936 VQI256:-721 SAY3072:-706 Yyc0:-699 GNB640:-650 STU0:-548 PpR0.2:-544 dc1:-540 ST1128:-533 Yyx2048:-521 PpR0:-472 Ytab20:-468 STU10:-438 e0:-416 VNU256:-408 ST1512:-404 ST10:-400 z10:-393 ST1256:-382 raw1:-370 VNU0:-359 VQS256:-351 VOFF256:-302 VNU512:-291 VQI0:-287 VQI512:-276 VQS0:-265 VQS512:-257 ST1384:-238 VOFF0:-227 SX0:-223 SDY1024:-219 VTU128:-212 VOFF512:-208 VDY0:-200 VNU384:-197 SAY3584:-189 VNU128:-185 VNU640:-182 VQI128:-178 VQI384:-170 VQS128:-167 SCUT0:-163 Yyx0:-159 ST1640:-155 VQS384:-148 VQI640:-144 VOFF128:-133 SX1024:-125 VQS640:-121 VOFF384:-117 SDY2048:-110 VOFF640:-99 SAY1024:-95 Yyq0:-91 VFK128:-87 dq1:-84 dc0:-80 VDV1024:-76 VDV2048:-72 VDV0:-68 GNB512:-57 SX2048:-53 VAV1024:-50 Yyp0:-42 VAV0:-19 SAY1536:0 SAY0:11 k1:15 dq0:56 sDV8:67 fold2:71 sDV12:101 sDV0:105 z0:113 SX3072:120 VE128:124 sAY0:128 k0:132 VUM0:158 sAV0:162 SSG0:166 VE0:177 SDY3072:184 VFK0:192 sDY8:203 VW116:207 VKX0:222 Ypool2512:226 PpR0.3:233 VEE256:237 PpR0.4:241 z11:245 VDV3072:252 VK0:256 VAV3072:260 VB224:264 VW224:271 VW10:275 VMK2048:283 VB248:298 VO10:313 sAV12:316 VK16:320 VW2s24:328 VMK0:332 Scf8:335 VO224:354 VB216:362 VMS0:366 SDI0:369 SRT0:373 sAY12:377 VNB768:384 VEE0:388 Syp128:392 sAV8:396 sAY8:400 VB256:411 VO116:415 VKX128:418 a01:422 SSG128:426 SXM0:430 um0:437 SDI128:445 SZV0:449 SZV256:471 VMS2048:475 count:483 Yyz0:486 Vtab20:490 VW20:498 VW28:501 SNB256:505 VW216:509 a02:513 um1:516 VW256:520 VW2s0:524 SXM256:539 SNB128:547 Gtab4096:569 SNB768:581 VO20:611 SXM384:615 SNB0:626 Vtab0:633 VUM8:637 VW232:645 VW240:656 Sjunk0:664 SRT256:667 VW248:671 VW2s32:675 VW2s40:679 VO232:683 VO240:686 SCUT128:690 Vtab2048:694 VNB896:716 VZV384:732 VpF10:739 Syq128:766 VpF1128:769 VNB384:796 Scf10:860 STHR0:898 Vpool20:939 YMK2048:962 Vpool1024:1060 Vpool0:1139 Yyl0:1143 YMK0:1150 Yyl512:1181 Scf9:1230 Syc128:1249 Syz128:1403"
PLAN.update(v="GVGV", y="FMFS", whole="00", place="-115 -134 175 244 41 -653 -401 160 713 354 629 -176 -58 99 522 721 393 251 -8 431 -81 114 -375 -359 -470 -157 -447 -161 912 -600 -592 -382 -77 0 45 248 480 568 419 412 820 709 1171 667 1095 1110 1057 1954 72 225 312 -84 503 465 -203 22 -27 198 -35 213 366 343 293 217 232 229 438 15 374 255 496 286 507 793 339 755 -474 -195 -481 -149 -451 -188 -20 469 492 278 683 633 -210 -62 -275 -39 -218 -42 -237 -153 -462 -100 -249 -107 -222 -69 -420 -65 -233 -73 -214 362 576 202 450 385 377 179 595 583 587 572 381 446 240 614 610 748 770 774 1358 1080 801 557 515 729 950 828 11 -146 396 1622 1652 1221 -126 19 -791 1603 -1558 -294 -3859 -3676 -3054 -2023 -1352 -2340 -1313 -2016 -283 -2012 -394 -1119 -1165 -123 -2344 -1951 38 -1542 290 320 -1737 389 -1917 -3577 103 -3584 -321 -3855 -3523 -3298 129 -1936 -813 328 -1913 -2111 -1726 -1730 -3310 -459 -1844 -1733 -31 -3500 -1909 -184 -1932 -1970 106 -3699 -130 -1939 297 -3695 -3649 -1924 -256 -3565 -1974 -1741 -3466 -3852 -3806 -104 -4092 -191 -241 -1966 -409 -3817 -833 206 -2848 -3260 -3355 -3306 -489 -325 -3363 454 698 488 -329 3 -527 -455 -138 -516 53 309 164 427 -539 -439 133 282 125 332 137 316 -142 335 -436 118 122 7 -168 -96 -1336 -1264 370 236 404 -810 732")
OPS, _names = plan(PLAN)
SEMAPHORES = ["cV", "cS", "cP", "cG", "sent"] + _names


def helpers(T, topo):
    pairs = {}
    for core in T.cores:
        spare = [c for c in topo.cores_of(core) if c not in T.cores and c not in pairs.values()]
        pairs[core] = min(spare, key=lambda c: (topo.die(c) != topo.die(core), abs(c - core)))
    return pairs


def engines(topo, src, dst, half):
    return sum(1 << e for e in topo.engines(src, dst)[NENG * half:NENG * (half + 1)])


def rank_program(g, core, T, topo):
    def ap(a):
        if not isref(a):
            return a
        v = T[a["ref"]][a["ix"]]
        return v.indirect(ap(a["off"])) if "off" in a else v

    folds = [op for op in OPS if op["kind"] == "fold"]
    helper = helpers(T, topo)
    rank = T.rank_of(core)
    if rank is None:
        for owner, c in helper.items():
            if c == core and folds:
                back = DstId(rid=topo.addr(owner)[0], pnc=topo.addr(owner)[1])
                for j, op in enumerate(folds):
                    sem, val = op["sig"]
                    g.wait_ge(T.sem[sem], val)
                    g.remote_dma_fused([RemoteDMATransfer(dst_ids=[back], dma_engine_mask=engines(topo, core, owner, (i + j) % 2),
                                                          remote_sem=T.sem[sem], src=ap(a), dst=ap(a))
                                        for i, a in enumerate(op["args"][::3])], local_sem=T.sem.sent)
                g.wait_ge(T.sem.sent, NENG * sum(len(op["args"]) // 3 for op in folds))
        return
    nxt = T.cores[(rank + 1) % len(T.cores)]
    rid, pid = topo.addr(nxt)[:2]
    aid = DstId(rid=topo.addr(helper[core])[0], pnc=topo.addr(helper[core])[1])
    Q = {"V": g.vector, "S": g.scalar, "P": g.tensor, "G": g, "Y": g.sync}
    final, sent, nf = {}, 0, 0
    for op in OPS:
        q, kind = Q[op["eng"]], op["kind"]
        for sem, val in op["waits"].items():
            q.wait_ge(T.sem[sem], val)
        sem, val = op["sig"]
        final[sem] = val
        if kind == "mm":
            for c in op["args"]:
                ins = q.matmul(ap(c[0]), ap(c[1]), ap(c[2]), c[3], c[4])
            ins.then_inc(T.sem[sem], 1)
            continue
        a = [ap(v) for v in op["args"]]
        if kind == "send":
            g.remote_dma_fused([RemoteDMATransfer(dst_ids=[DstId(rid=rid, pnc=pid)], dma_engine_mask=engines(topo, core, nxt, 0),
                                                  remote_sem=T.sem[sem], srcs=[a[1], a[2]], dsts=[a[0]], alu_op=1)], local_sem=T.sem.sent)
            sent += NENG
            continue
        if kind == "fold":
            g.remote_dma_fused([RemoteDMATransfer(dst_ids=[aid], dma_engine_mask=engines(topo, core, helper[core], (i // 3 + nf) % 2),
                                                  remote_sem=T.sem[sem], srcs=[a[i + 1], a[i + 2]], dsts=[a[i]], alu_op=2)
                                for i in range(0, len(a), 3)], local_sem=T.sem.sent)
            sent += NENG * (len(a) // 3)
            nf += 1
            continue
        if kind == "dma":
            whole = [T[v["ref"]][:] if v["ref"] in ("wt", "de") else w for v, w in zip(op["args"], a)]
            q.dma_start(whole[0], whole[1]).then_inc(T.sem[sem], 16)
            continue
        if kind == "cp":
            ins = q.tensor_copy(a[0], a[1])
        elif kind == "tt":
            ins = q.tensor_tensor(a[0], a[1], a[2], a[3])
        elif kind == "ts":
            ins = q.tensor_scalar(*a[:5]) if a[5] is None else q.tensor_scalar(*a)
        elif kind == "scan":
            ins = q.tensor_tensor_scan(a[0], a[1], a[2], -1.0, a[3], a[4])
        elif kind == "ms":
            ins = q.memset(a[0], a[1])
        elif kind == "act":
            ins = q.activation(a[0], a[1], a[2], bias=a[3], scale=a[4], accum_out=ap(op["accum"]))
        elif kind == "iota":
            if dtype(op["args"][0]["ref"]) == I:
                ins = g.iota(a[0], a[1], a[2], a[3])
            else:
                ins = g.iota(a[0], a[1], a[2], a[3], allow_small_or_imprecise_dtypes=True)
        elif a[2]:
            ins = g.affine_select(a[0], a[1], [[-1, 128]], ALU.is_equal, 0.0, 0, 1)
        else:
            ins = g.affine_select(a[0], a[1], [[0, op["args"][0]["n"]]], ALU.is_equal, 0.0, 0, 0)
        ins.then_inc(T.sem[sem], 1)
    g.wait_ge(T.sem.sent, sent)
    for sem, val in final.items():
        g.wait_ge(T.sem[sem], val)
